import numpy as np
import ml_dtypes


def mxq(x, axis, fmt="e4m3"):
    dtype, down = {"e4m3": (ml_dtypes.float8_e4m3fn, 7), "e5m2": (ml_dtypes.float8_e5m2, 14)}[fmt]
    v = np.moveaxis(np.asarray(x, np.float32).astype(ml_dtypes.bfloat16).astype(np.float64), axis, -1)
    blocks = v.reshape(v.shape[:-1] + (-1, 32))
    amax = np.abs(blocks).max(-1, keepdims=True)
    byte = np.maximum(np.where(amax > 0, np.frexp(amax)[1] - 1 + 127, 0) - down, 1)
    scale = np.exp2(byte - 127.0)
    codes = (blocks / scale).astype(np.float32).astype(dtype).astype(np.float64)
    return np.moveaxis((codes * scale).reshape(v.shape), -1, axis)


WIDE = False


def mx_kscale(k):
    if not WIDE:
        return np.ones(k)
    levels = np.array([10, -10, 5, -5, 0])
    if k % 512:
        return np.exp2(np.random.permutation(np.resize(levels, k // 32))).repeat(32)
    a = np.empty((k // 512, 16))
    for p in range(k // 512):
        a[p, :8] = np.random.permutation(np.resize(levels, 8))
        for g in range(8):
            far = levels[np.abs(levels - a[p, g]) >= 10]
            a[p, g + 8] = far[np.random.randint(len(far))]
    return np.exp2(a.ravel()).repeat(32)


def f64(x):
    return np.asarray(x).astype(np.float64)


def striped(idx):
    return np.tile(np.asarray(idx).reshape(-1, 16).T, (8, 1)).astype(np.uint16)


def unstriped(offs):
    return offs[:16].T.reshape(-1).astype(np.int64)


E2M1 = np.array([0.0, 0.5, 1.0, 1.5, 2.0, 3.0, 4.0, 6.0, -0.0, -0.5, -1.0, -1.5, -2.0, -3.0, -4.0, -6.0])


def pack_weight(w, fmt):
    k, n = w.shape
    w = f64(np.asarray(w, np.float32).astype(ml_dtypes.bfloat16)).reshape(k // 32, 32, n)
    amax = np.abs(w).max(1)
    if fmt == "e4m3":
        byte = np.frexp(amax)[1] - 1 + 127 - 7
    else:
        mant, ex = np.frexp(amax / 6.0)
        byte = np.where(mant > 0.5, ex, ex - 1) + 127
    byte = np.clip(np.where(amax > 0, byte, 1), 1, 254)
    scaled = (w * np.exp2(127.0 - byte)[:, None, :]).reshape(k, n).astype(np.float32)
    by_word = np.ascontiguousarray(scaled.reshape(k // 512, 128, 4, n).transpose(0, 1, 3, 2))
    if fmt == "e4m3":
        words = by_word.astype(ml_dtypes.float8_e4m3fn).view(np.uint8)
    else:
        c = by_word.astype(ml_dtypes.float4_e2m1fn).view(np.uint8) & 0xF
        words = (c[..., 0::2] | (c[..., 1::2] << 4)).reshape(k // 512, 128, 2 * n)
    return np.ascontiguousarray(words), np.ascontiguousarray(byte.astype(np.uint8).reshape(k // 512, 16, n))


def unpack_weight(words, scales, fmt):
    g, _, n = scales.shape
    words = np.ascontiguousarray(words).reshape(g, 128, n, -1)
    if fmt == "e4m3":
        vals = words.view(ml_dtypes.float8_e4m3fn).astype(np.float64)
    else:
        nib = np.empty((g, 128, n, 4), np.uint8)
        nib[..., 0::2] = words & 0xF
        nib[..., 1::2] = words >> 4
        vals = E2M1[nib]
    vals = vals * np.repeat(np.exp2(scales.astype(np.float64) - 127.0), 8, axis=1)[..., None]
    return vals.transpose(0, 1, 3, 2).reshape(g * 512, n)


K, T, I, F, E = 512, 2048, 512, 512, 256


def setup_inputs():
    n = np.random.standard_normal
    idx = np.random.permutation(T)[:I]
    fk = mx_kscale(K)
    ff = mx_kscale(F)
    tokp = pack_weight(n((K, T)) / fk[:, None], "e4m3")
    return {
        "tok_words": tokp[0],
        "tok_scales": tokp[1],
        "wa": (n((K, F)) * 1 / np.sqrt(K) * fk[:, None] * ff).astype(np.float32),
        "wb": (n((F, E)) * 1 / np.sqrt(F) / ff[:, None]).astype(np.float32),
        "rw": (np.random.uniform(0.2, 1.0, (1, I))).astype(np.float32),
        "res": (n((E, T)) * 0.5).astype(np.float32),
        "offs": striped(idx),
    }


def reference(tok_words, tok_scales, wa, wb, rw, res, offs):
    idx = unstriped(offs)
    toku = unpack_weight(tok_words, tok_scales, "e4m3")
    waq = mxq(f64(wa), 0, "e4m3")
    tokidxg = toku[:, idx]
    z = waq.T @ tokidxg
    h1 = np.maximum(z, 0.0)
    wbq = mxq(f64(wb), 0, "e4m3")
    h1q = mxq(h1, 0, "e4m3")
    o = wbq.T @ h1q
    x = o * f64(rw)
    xf = np.zeros((E, T))
    xf[:, idx] = x
    y = f64(res) + xf
    return y

@@ -1,0 +1,215 @@
+from contextlib import ExitStack
+
+import concourse.mybir as mybir
+
+K, T, I, F, E = 512, 2048, 512, 512, 256
+FLOPS = 2 * K * F * I + 2 * F * E * I
+
+F32 = mybir.dt.float32
+BF16 = mybir.dt.bfloat16
+I32 = mybir.dt.int32
+U32 = mybir.dt.uint32
+U16 = mybir.dt.uint16
+U8 = mybir.dt.uint8
+FP8X4 = mybir.dt.float8_e4m3fn_x4
+ACT = mybir.ActivationFunctionType
+ALU = mybir.AluOpType
+
+P = 128
+PACK = 4
+HALF = 256
+CHUNK = 128
+OUT_COLS = 512
+
+
+def tile_attend_depthffn_kernel(tc, tok_words, tok_scales, wa, wb, rw, res, offs, out):
+    nc = tc.nc
+    with ExitStack() as ctx:
+        keep = ctx.enter_context(tc.tile_pool(name="keep", bufs=1))
+        psum = ctx.enter_context(tc.psum_pool(name="psum", bufs=1))
+
+        offsets = keep.tile([P, I // 16], U16, name="offsets")
+        nc.sync.dma_start(offsets[:], offs)
+
+        rw_cols = keep.tile([P, PACK], F32, name="rw_cols")
+
+        wa_raw = keep.tile([P, PACK, F], F32, name="wa_raw")
+        nc.sync.dma_start(wa_raw[:], wa.rearrange("(p j) f -> p j f", j=PACK))
+
+        scale_pool = keep.tile([P, T], U8, name="scale_pool", align_bytes=64)
+        nc.gpsimd.memset(scale_pool[:].bitcast(I32), 0)
+        for q in range(4):
+            nc.sync.dma_start(
+                scale_pool[32 * q : 32 * q + 4, :].bitcast(I32),
+                tok_scales[0, 4 * q : 4 * q + 4, :].bitcast(I32),
+            )
+        nc.sync.dma_start(rw_cols[:], rw.rearrange("o (p j) -> (o p) j", j=PACK))
+        word_pool = keep.tile([P, T], U32, name="word_pool", align_bytes=64)
+        nc.sync.dma_start(
+            word_pool[:].bitcast(I32),
+            tok_words[0].rearrange("p t r -> p (t r)").bitcast(I32),
+        )
+        wb_raw = keep.tile([P, PACK, E], F32, name="wb_raw")
+        nc.sync.dma_start(wb_raw[:], wb.rearrange("(p j) e -> p j e", j=PACK))
+        res_head = keep.tile([P, OUT_COLS], F32, name="res_head")
+        nc.sync.dma_start(res_head[:], res[0:P, 0:OUT_COLS])
+        res_turn = keep.tile([P, T - OUT_COLS], F32, name="res_turn")
+        res_last = keep.tile([P, T], F32, name="res_last")
+        nc.sync.dma_start(res_last[:], res[P:E, :])
+        nc.sync.dma_start(res_turn[:], res[0:P, OUT_COLS:T])
+
+        xf = []
+        for g in range(E // P):
+            w = keep.tile([P, T], F32, name=f"xf{g}")
+            nc.vector.memset(w[:], 0.0)
+            xf.append(w)
+
+        diff = keep.tile([P, P], F32, name="diff")
+        nc.gpsimd.iota(diff[:], [[1, P]], base=0, channel_multiplier=-1, allow_small_or_imprecise_dtypes=True)
+        dist = keep.tile([P, P], F32, name="dist")
+        nc.scalar.activation(dist[:], diff[:], ACT.Abs)
+        ident = keep.tile([P, P], F32, name="ident")
+        nc.scalar.activation(ident[:], dist[:], ACT.Relu, bias=1.0, scale=-1.0)
+
+        wa_src = wa_raw[:].rearrange("p j (m t) -> p m t j", t=PACK)
+        wa_bf = []
+        for u in range(2):
+            b = keep.tile([P, 2, P, PACK], BF16, name=f"wa_bf{u}", align_bytes=64)
+            dst = b[:].rearrange("p t m j -> p m t j")
+            if u == 0:
+                nc.vector.tensor_copy(dst, wa_src[:, :, 0:2, :])
+            else:
+                nc.scalar.copy(dst, wa_src[:, :, 2:4, :])
+            wa_bf.append(b)
+
+        tok_scale_g = keep.tile([P, I], U8, name="tok_scale_g", align_bytes=64)
+        nc.vector.tensor_copy(tok_scale_g[:], scale_pool[:].indirect(offsets[:]))
+
+        wa_codes = keep.tile([P, F], U32, name="wa_codes", align_bytes=64)
+        wa_scales = keep.tile([P, F], U8, name="scale_pool", align_bytes=64)
+        for u in range(2):
+            cols = slice(2 * P * u, 2 * P * (u + 1))
+            nc.vector.quantize_mx(out=wa_codes[:, cols].bitcast(FP8X4), scales=wa_scales[:, cols], in_=wa_bf[u][:].rearrange("p t m j -> p (t m j)"))
+
+        rw_ps = psum.tile([P, PACK, P], F32, name="o_ps3")
+        for j in range(PACK):
+            nc.tensor.transpose(rw_ps[:, j, :], rw_cols[:, j : j + 1].to_broadcast([P, P]), ident[:])
+        rw_rows = keep.tile([P, P, PACK], F32, name="rw_rows")
+        nc.scalar.copy(rw_rows[:], rw_ps[:].rearrange("p j n -> p n j"))
+        rw_flat = rw_rows[:].rearrange("p n j -> p (n j)")
+
+        tok_g = []
+        for h in range(2):
+            g = keep.tile([P, HALF], U32, name=f"tok_g{h}", align_bytes=64)
+            nc.vector.tensor_copy(g[:], word_pool[:].indirect(offsets[:, 16 * h : 16 * (h + 1)]))
+            tok_g.append(g)
+
+        h_bf = []
+        z_ps = []
+        for c in range(I // CHUNK):
+            z = psum.tile([P, PACK, CHUNK], F32, name=f"z_ps{c}")
+            h, lo = divmod(c * CHUNK, HALF)
+            for t in range(PACK):
+                nc.tensor.matmul_mx(
+                    out=z[:, t, :],
+                    lhsT=wa_codes[:, t * P : (t + 1) * P].bitcast(FP8X4),
+                    lhsT_scale=wa_scales[:, t * P : (t + 1) * P],
+                    rhs=tok_g[h][:, lo : lo + CHUNK].bitcast(FP8X4),
+                    rhs_scale=tok_scale_g[:, c * CHUNK : (c + 1) * CHUNK],
+                    start=True,
+                    stop=True,
+                )
+            z_ps.append(z)
+            if c < 3:
+                hb = keep.tile([P, CHUNK, PACK], BF16, name=f"h_bf{c}", align_bytes=64)
+                h_bf.append(hb)
+                nc.scalar.activation(hb[:], z[:].rearrange("p t i -> p i t"), ACT.Relu)
+
+        wb_bf = keep.tile([P, E, PACK], BF16, name="wb_bf", align_bytes=64)
+        nc.vector.tensor_copy(wb_bf[:], wb_raw[:].rearrange("p j e -> p e j"))
+        wb_codes = keep.tile([P, E], U32, name="wb_codes", align_bytes=64)
+        wb_scales = keep.tile([P, E], U8, name="wb_scales", align_bytes=64)
+
+        h_codes = keep.tile([P, I], U32, name="h_codes", align_bytes=64)
+        h_scales = keep.tile([P, I], U8, name="h_scales", align_bytes=64)
+
+        def quantise_h(c):
+            cols = slice(c * CHUNK, (c + 1) * CHUNK)
+            nc.vector.quantize_mx(
+                out=h_codes[:, cols].bitcast(FP8X4),
+                scales=h_scales[:, cols],
+                in_=h_bf[c][:].rearrange("p i t -> p (i t)"),
+            )
+
+        def second_layer(g, lo, width, bank):
+            o = psum.tile([P, width], F32, name=bank)
+            nc.tensor.matmul_mx(
+                out=o[:],
+                lhsT=wb_codes[:, g * P : (g + 1) * P].bitcast(FP8X4),
+                lhsT_scale=wb_scales[:, g * P : (g + 1) * P],
+                rhs=h_codes[:, lo : lo + width].bitcast(FP8X4),
+                rhs_scale=h_scales[:, lo : lo + width],
+                start=True,
+                stop=True,
+            )
+            return o
+
+        o_half = [keep.tile([P, HALF], F32, name=f"o_sb{h}") for h in range(2)]
+        quantise_h(0)
+        nc.vector.quantize_mx(out=wb_codes[:].bitcast(FP8X4), scales=wb_scales[:], in_=wb_bf[:].rearrange("p e j -> p (e j)"))
+        quantise_h(1)
+        nc.scalar.copy(o_half[0][:], second_layer(0, 0, HALF, "o_ps0")[:])
+        h_bf.append(keep.tile([P, CHUNK, PACK], BF16, name="h_bf1", align_bytes=64))
+        nc.vector.tensor_scalar_max(h_bf[3][:], z_ps[3][:].rearrange("p t i -> p i t"), 0.0)
+        quantise_h(2)
+        quantise_h(3)
+        nc.scalar.copy(o_half[1][:], second_layer(0, HALF, HALF, "o_ps2")[:])
+        o_last_ps = second_layer(1, 0, I, "o_ps3")
+
+        n_turn = (T - OUT_COLS) // OUT_COLS
+        turned = []
+        for b in range(n_turn):
+            acc = psum.tile([P, PACK, P], F32, name=f"z_ps{b}")
+            for k in range(PACK):
+                lo = b * OUT_COLS + k * P
+                nc.tensor.matmul(acc[:, k, :], res_turn[:, lo : lo + P], ident[:], start=(k == 0), stop=False, is_transpose=True)
+            turned.append(acc)
+
+        for h in range(2):
+            nc.vector.tensor_tensor(
+                xf[0][:].indirect(offsets[:, 16 * h : 16 * (h + 1)]),
+                o_half[h][:],
+                rw_flat[:, h * HALF : (h + 1) * HALF],
+                ALU.mult,
+            )
+        o_last = keep.tile([P, I], F32, name="o_sb1")
+        nc.scalar.copy(o_last[:], o_last_ps[:])
+
+        y = keep.tile([P, OUT_COLS], F32, name="y_head")
+        nc.vector.tensor_tensor(y[:], xf[0][:, 0:OUT_COLS], res_head[:], ALU.add)
+        nc.sync.dma_start(out[0:P, 0:OUT_COLS], y[:])
+
+        nc.vector.tensor_tensor(xf[1][:].indirect(offsets[:]), o_last[:], rw_flat, ALU.mult)
+
+        sums = []
+        for b in range(n_turn):
+            for k in range(PACK):
+                lo = (b + 1) * OUT_COLS + k * P
+                nc.tensor.matmul(turned[b][:, k, :], xf[0][:, lo : lo + P], ident[:], start=False, stop=(k == PACK - 1), is_transpose=True)
+            sm = keep.tile([P, PACK, P], F32, name=f"sum_t{b}")
+            nc.scalar.copy(sm[:], turned[b][:])
+            sums.append(sm)
+        for b in range(n_turn):
+            back = psum.tile([P, OUT_COLS], F32, name=("z_ps3", "o_ps1", "o_ps2")[b])
+            for k in range(PACK):
+                nc.tensor.transpose(back[:, k * P : (k + 1) * P], sums[b][:, k, :], ident[:])
+            yb = keep.tile([P, OUT_COLS], F32, name=f"y_turn{b}")
+            nc.scalar.copy(yb[:], back[:])
+            nc.scalar.dma_start(out[0:P, (b + 1) * OUT_COLS : (b + 2) * OUT_COLS], yb[:])
+
+        edges = [0, 256, 768, 1280, 1792, 2048]
+        for n in range(len(edges) - 1):
+            cols = slice(edges[n], edges[n + 1])
+            yl = keep.tile([P, edges[n + 1] - edges[n]], F32, name=f"y_last{n}")
+            nc.vector.tensor_tensor(yl[:], xf[1][:, cols], res_last[:, cols], ALU.add)
+            nc.sync.dma_start(out[P:E, cols], yl[:])

@@ -19,7 +19,8 @@ P = 128
 PACK = 4
 HALF = 256
 CHUNK = 128
-OUT_COLS = 512
+POOL_COLS = [(0, 384), (384, 768), (768, 1152)]
+TURN_COLS = [(1152, 1536), (1536, 2048)]
 
 
 def tile_attend_depthffn_kernel(tc, tok_words, tok_scales, wa, wb, rw, res, offs, out):
@@ -38,10 +39,10 @@ def tile_attend_depthffn_kernel(tc, tok_words, tok_scales, wa, wb, rw, res, offs
 
         scale_pool = keep.tile([P, T], U8, name="scale_pool", align_bytes=64)
         nc.gpsimd.memset(scale_pool[:].bitcast(I32), 0)
-        for q in range(4):
+        for r in range(4):
             nc.sync.dma_start(
-                scale_pool[32 * q : 32 * q + 4, :].bitcast(I32),
-                tok_scales[0, 4 * q : 4 * q + 4, :].bitcast(I32),
+                scale_pool[r:P:32, :].bitcast(I32),
+                tok_scales[0, r:16:4, :].bitcast(I32),
             )
         nc.sync.dma_start(rw_cols[:], rw.rearrange("o (p j) -> (o p) j", j=PACK))
         word_pool = keep.tile([P, T], U32, name="word_pool", align_bytes=64)
@@ -51,12 +52,10 @@ def tile_attend_depthffn_kernel(tc, tok_words, tok_scales, wa, wb, rw, res, offs
         )
         wb_raw = keep.tile([P, PACK, E], F32, name="wb_raw")
         nc.sync.dma_start(wb_raw[:], wb.rearrange("(p j) e -> p j e", j=PACK))
-        res_head = keep.tile([P, OUT_COLS], F32, name="res_head")
-        nc.sync.dma_start(res_head[:], res[0:P, 0:OUT_COLS])
-        res_turn = keep.tile([P, T - OUT_COLS], F32, name="res_turn")
+        res_first = keep.tile([P, T], F32, name="res_first")
         res_last = keep.tile([P, T], F32, name="res_last")
+        nc.sync.dma_start(res_first[:], res[0:P, :])
         nc.sync.dma_start(res_last[:], res[P:E, :])
-        nc.sync.dma_start(res_turn[:], res[0:P, OUT_COLS:T])
 
         xf = []
         for g in range(E // P):
@@ -71,15 +70,15 @@ def tile_attend_depthffn_kernel(tc, tok_words, tok_scales, wa, wb, rw, res, offs
         ident = keep.tile([P, P], F32, name="ident")
         nc.scalar.activation(ident[:], dist[:], ACT.Relu, bias=1.0, scale=-1.0)
 
-        wa_src = wa_raw[:].rearrange("p j (m t) -> p m t j", t=PACK)
+        wa_src = wa_raw[:].rearrange("p j (m t) -> p m j t", t=PACK)
         wa_bf = []
         for u in range(2):
             b = keep.tile([P, 2, P, PACK], BF16, name=f"wa_bf{u}", align_bytes=64)
-            dst = b[:].rearrange("p t m j -> p m t j")
+            dst = b[:].rearrange("p t m j -> p m j t")
             if u == 0:
-                nc.vector.tensor_copy(dst, wa_src[:, :, 0:2, :])
+                nc.vector.tensor_copy(dst, wa_src[:, :, :, 0:2])
             else:
-                nc.scalar.copy(dst, wa_src[:, :, 2:4, :])
+                nc.scalar.copy(dst, wa_src[:, :, :, 2:4])
             wa_bf.append(b)
 
         tok_scale_g = keep.tile([P, I], U8, name="tok_scale_g", align_bytes=64)
@@ -126,7 +125,7 @@ def tile_attend_depthffn_kernel(tc, tok_words, tok_scales, wa, wb, rw, res, offs
                 nc.scalar.activation(hb[:], z[:].rearrange("p t i -> p i t"), ACT.Relu)
 
         wb_bf = keep.tile([P, E, PACK], BF16, name="wb_bf", align_bytes=64)
-        nc.vector.tensor_copy(wb_bf[:], wb_raw[:].rearrange("p j e -> p e j"))
+        nc.vector.tensor_copy(wb_bf[:].rearrange("p (c i) j -> p c j i", i=PACK), wb_raw[:].rearrange("p j (c i) -> p c j i", i=PACK))
         wb_codes = keep.tile([P, E], U32, name="wb_codes", align_bytes=64)
         wb_scales = keep.tile([P, E], U8, name="wb_scales", align_bytes=64)
 
@@ -166,46 +165,47 @@ def tile_attend_depthffn_kernel(tc, tok_words, tok_scales, wa, wb, rw, res, offs
         nc.scalar.copy(o_half[1][:], second_layer(0, HALF, HALF, "o_ps2")[:])
         o_last_ps = second_layer(1, 0, I, "o_ps3")
 
-        n_turn = (T - OUT_COLS) // OUT_COLS
         turned = []
-        for b in range(n_turn):
-            acc = psum.tile([P, PACK, P], F32, name=f"z_ps{b}")
-            for k in range(PACK):
-                lo = b * OUT_COLS + k * P
-                nc.tensor.matmul(acc[:, k, :], res_turn[:, lo : lo + P], ident[:], start=(k == 0), stop=False, is_transpose=True)
+        for b, (lo, hi) in enumerate(TURN_COLS):
+            acc = psum.tile([P, hi - lo], F32, name=f"z_ps{b}")
+            for k in range((hi - lo) // P):
+                nc.tensor.matmul(acc[:, k * P : (k + 1) * P], res_first[:, lo + k * P : lo + (k + 1) * P], ident[:], start=(k == 0), stop=False, is_transpose=True)
             turned.append(acc)
 
-        for h in range(2):
+        def scatter_first(h):
             nc.vector.tensor_tensor(
                 xf[0][:].indirect(offsets[:, 16 * h : 16 * (h + 1)]),
                 o_half[h][:],
                 rw_flat[:, h * HALF : (h + 1) * HALF],
                 ALU.mult,
             )
-        o_last = keep.tile([P, I], F32, name="o_sb1")
-        nc.scalar.copy(o_last[:], o_last_ps[:])
 
-        y = keep.tile([P, OUT_COLS], F32, name="y_head")
-        nc.vector.tensor_tensor(y[:], xf[0][:, 0:OUT_COLS], res_head[:], ALU.add)
-        nc.sync.dma_start(out[0:P, 0:OUT_COLS], y[:])
+        scatter_first(0)
+        x_last = keep.tile([P, I], F32, name="x_last")
+        nc.vector.tensor_tensor(x_last[:], o_last_ps[:], rw_flat, ALU.mult)
+        scatter_first(1)
+        nc.vector.tensor_copy(xf[1][:].indirect(offsets[:]), x_last[:])
 
-        nc.vector.tensor_tensor(xf[1][:].indirect(offsets[:]), o_last[:], rw_flat, ALU.mult)
+        for n, (lo, hi) in enumerate(POOL_COLS):
+            y = keep.tile([P, hi - lo], F32, name=f"y_pool{n}")
+            nc.gpsimd.tensor_tensor(y[:], xf[0][:, lo:hi], res_first[:, lo:hi], ALU.add)
+            nc.sync.dma_start(out[0:P, lo:hi], y[:])
 
         sums = []
-        for b in range(n_turn):
-            for k in range(PACK):
-                lo = (b + 1) * OUT_COLS + k * P
-                nc.tensor.matmul(turned[b][:, k, :], xf[0][:, lo : lo + P], ident[:], start=False, stop=(k == PACK - 1), is_transpose=True)
-            sm = keep.tile([P, PACK, P], F32, name=f"sum_t{b}")
+        for b, (lo, hi) in enumerate(TURN_COLS):
+            blocks = (hi - lo) // P
+            for k in range(blocks):
+                nc.tensor.matmul(turned[b][:, k * P : (k + 1) * P], xf[0][:, lo + k * P : lo + (k + 1) * P], ident[:], start=False, stop=(k == blocks - 1), is_transpose=True)
+            sm = keep.tile([P, hi - lo], F32, name=f"sum_t{b}")
             nc.scalar.copy(sm[:], turned[b][:])
             sums.append(sm)
-        for b in range(n_turn):
-            back = psum.tile([P, OUT_COLS], F32, name=("z_ps3", "o_ps1", "o_ps2")[b])
-            for k in range(PACK):
-                nc.tensor.transpose(back[:, k * P : (k + 1) * P], sums[b][:, k, :], ident[:])
-            yb = keep.tile([P, OUT_COLS], F32, name=f"y_turn{b}")
+        for b, (lo, hi) in enumerate(TURN_COLS):
+            back = psum.tile([P, hi - lo], F32, name=f"z_ps{2 + b}")
+            for k in range((hi - lo) // P):
+                nc.tensor.transpose(back[:, k * P : (k + 1) * P], sums[b][:, k * P : (k + 1) * P], ident[:])
+            yb = keep.tile([P, hi - lo], F32, name=f"y_turn{b}")
             nc.scalar.copy(yb[:], back[:])
-            nc.scalar.dma_start(out[0:P, (b + 1) * OUT_COLS : (b + 2) * OUT_COLS], yb[:])
+            nc.scalar.dma_start(out[0:P, lo:hi], yb[:])
 
         edges = [0, 256, 768, 1280, 1792, 2048]
         for n in range(len(edges) - 1):

@@ -30,12 +30,12 @@ def tile_attend_depthffn_kernel(tc, tok_words, tok_scales, wa, wb, rw, res, offs
         psum = ctx.enter_context(tc.psum_pool(name="psum", bufs=1))
 
         offsets = keep.tile([P, I // 16], U16, name="offsets")
-        nc.sync.dma_start(offsets[:], offs)
 
         rw_cols = keep.tile([P, PACK], F32, name="rw_cols")
 
         wa_raw = keep.tile([P, PACK, F], F32, name="wa_raw")
         nc.sync.dma_start(wa_raw[:], wa.rearrange("(p j) f -> p j f", j=PACK))
+        nc.sync.dma_start(offsets[:], offs)
 
         scale_pool = keep.tile([P, T], U8, name="scale_pool", align_bytes=64)
         nc.gpsimd.memset(scale_pool[:].bitcast(I32), 0)
@@ -207,7 +207,7 @@ def tile_attend_depthffn_kernel(tc, tok_words, tok_scales, wa, wb, rw, res, offs
             nc.scalar.copy(yb[:], back[:])
             nc.scalar.dma_start(out[0:P, lo:hi], yb[:])
 
-        edges = [0, 256, 768, 1280, 1792, 2048]
+        edges = [0, 128, 384, 896, 1408, 1920, 2048]
         for n in range(len(edges) - 1):
             cols = slice(edges[n], edges[n + 1])
             yl = keep.tile([P, edges[n + 1] - edges[n]], F32, name=f"y_last{n}")

@@ -57,11 +57,8 @@ def tile_attend_depthffn_kernel(tc, tok_words, tok_scales, wa, wb, rw, res, offs
         nc.sync.dma_start(res_first[:], res[0:P, :])
         nc.sync.dma_start(res_last[:], res[P:E, :])
 
-        xf = []
-        for g in range(E // P):
-            w = keep.tile([P, T], F32, name=f"xf{g}")
-            nc.vector.memset(w[:], 0.0)
-            xf.append(w)
+        xf = [keep.tile([P, T], F32, name="xf0")]
+        nc.vector.memset(xf[0][:], 0.0)
 
         diff = keep.tile([P, P], F32, name="diff")
         nc.gpsimd.iota(diff[:], [[1, P]], base=0, channel_multiplier=-1, allow_small_or_imprecise_dtypes=True)
@@ -162,6 +159,8 @@ def tile_attend_depthffn_kernel(tc, tok_words, tok_scales, wa, wb, rw, res, offs
         nc.vector.tensor_scalar_max(h_bf[3][:], z_ps[3][:].rearrange("p t i -> p i t"), 0.0)
         quantise_h(2)
         quantise_h(3)
+        xf.append(keep.tile([P, T], F32, name="h_bf2", align_bytes=64))
+        nc.gpsimd.memset(xf[1][:], 0.0)
         nc.scalar.copy(o_half[1][:], second_layer(0, HALF, HALF, "o_ps2")[:])
         o_last_ps = second_layer(1, 0, I, "o_ps3")
 

@@ -1,6 +1,7 @@
 from contextlib import ExitStack
 
 import concourse.mybir as mybir
+from concourse.masks import make_identity
 
 K, T, I, F, E = 512, 2048, 512, 512, 256
 FLOPS = 2 * K * F * I + 2 * F * E * I
@@ -19,8 +20,10 @@ P = 128
 PACK = 4
 HALF = 256
 CHUNK = 128
-POOL_COLS = [(0, 384), (384, 768), (768, 1152)]
-TURN_COLS = [(1152, 1536), (1536, 2048)]
+POOL_COLS = [(0, 384), (384, 896), (896, 1152)]
+TURN_COLS = [(1152, 1408), (1408, 1792), (1792, 2048)]
+CAST_SPLIT = 48
+LAST_EDGES = [0, 128, 384, 896, 1408, 1920, 2048]
 
 
 def tile_attend_depthffn_kernel(tc, tok_words, tok_scales, wa, wb, rw, res, offs, out):
@@ -33,7 +36,7 @@ def tile_attend_depthffn_kernel(tc, tok_words, tok_scales, wa, wb, rw, res, offs
 
         rw_cols = keep.tile([P, PACK], F32, name="rw_cols")
 
-        wa_raw = keep.tile([P, PACK, F], F32, name="wa_raw")
+        wa_raw = keep.tile([P, PACK, F], F32, name="wa_raw", align_bytes=64)
         nc.sync.dma_start(wa_raw[:], wa.rearrange("(p j) f -> p j f", j=PACK))
         nc.sync.dma_start(offsets[:], offs)
 
@@ -57,76 +60,63 @@ def tile_attend_depthffn_kernel(tc, tok_words, tok_scales, wa, wb, rw, res, offs
         nc.sync.dma_start(res_first[:], res[0:P, :])
         nc.sync.dma_start(res_last[:], res[P:E, :])
 
-        xf = [keep.tile([P, T], F32, name="xf0")]
-        nc.vector.memset(xf[0][:], 0.0)
-
-        diff = keep.tile([P, P], F32, name="diff")
-        nc.gpsimd.iota(diff[:], [[1, P]], base=0, channel_multiplier=-1, allow_small_or_imprecise_dtypes=True)
-        dist = keep.tile([P, P], F32, name="dist")
-        nc.scalar.activation(dist[:], diff[:], ACT.Abs)
+        xf = [keep.tile([P, T], F32, name=f"xf{g}") for g in range(2)]
         ident = keep.tile([P, P], F32, name="ident")
-        nc.scalar.activation(ident[:], dist[:], ACT.Relu, bias=1.0, scale=-1.0)
+        nc.vector.memset(ident[:], 0.0)
+        nc.vector.memset(xf[0][:], 0.0)
+        nc.vector.memset(xf[1][:, 0 : T // 2], 0.0)
+        make_identity(nc, ident[:], nomemset=True)
+        nc.gpsimd.memset(xf[1][:, T // 2 : T], 0.0)
 
         wa_src = wa_raw[:].rearrange("p j (m t) -> p m j t", t=PACK)
-        wa_bf = []
-        for u in range(2):
-            b = keep.tile([P, 2, P, PACK], BF16, name=f"wa_bf{u}", align_bytes=64)
-            dst = b[:].rearrange("p t m j -> p m j t")
-            if u == 0:
-                nc.vector.tensor_copy(dst, wa_src[:, :, :, 0:2])
-            else:
-                nc.scalar.copy(dst, wa_src[:, :, :, 2:4])
-            wa_bf.append(b)
+        wa_bf = keep.tile([P, PACK, P, PACK], BF16, name="wa_bf", align_bytes=64)
+        wa_dst = wa_bf[:].rearrange("p t m j -> p m j t")
+        nc.vector.tensor_copy(wa_dst[:, 0:CAST_SPLIT], wa_src[:, 0:CAST_SPLIT])
+        nc.scalar.copy(wa_dst[:, CAST_SPLIT:P], wa_src[:, CAST_SPLIT:P])
 
-        tok_scale_g = keep.tile([P, I], U8, name="tok_scale_g", align_bytes=64)
-        nc.vector.tensor_copy(tok_scale_g[:], scale_pool[:].indirect(offsets[:]))
-
-        wa_codes = keep.tile([P, F], U32, name="wa_codes", align_bytes=64)
-        wa_scales = keep.tile([P, F], U8, name="scale_pool", align_bytes=64)
-        for u in range(2):
-            cols = slice(2 * P * u, 2 * P * (u + 1))
-            nc.vector.quantize_mx(out=wa_codes[:, cols].bitcast(FP8X4), scales=wa_scales[:, cols], in_=wa_bf[u][:].rearrange("p t m j -> p (t m j)"))
-
-        rw_ps = psum.tile([P, PACK, P], F32, name="o_ps3")
+        rw_ps = psum.tile([P, PACK, P], F32, name="o_ps0")
         for j in range(PACK):
             nc.tensor.transpose(rw_ps[:, j, :], rw_cols[:, j : j + 1].to_broadcast([P, P]), ident[:])
         rw_rows = keep.tile([P, P, PACK], F32, name="rw_rows")
         nc.scalar.copy(rw_rows[:], rw_ps[:].rearrange("p j n -> p n j"))
         rw_flat = rw_rows[:].rearrange("p n j -> p (n j)")
 
-        tok_g = []
+        tok_scale_g = keep.tile([P, I], U8, name="tok_scale_g", align_bytes=64)
+        nc.vector.tensor_copy(tok_scale_g[:], scale_pool[:].indirect(offsets[:]))
+
+        wa_codes = keep.tile([P, F], U32, name="wa_codes", align_bytes=64)
+        wa_scales = keep.tile([P, F], U8, name="scale_pool", align_bytes=64)
+        nc.vector.quantize_mx(out=wa_codes[:].bitcast(FP8X4), scales=wa_scales[:], in_=wa_bf[:].rearrange("p t m j -> p (t m j)"))
+
+        tok_g = keep.tile([P, I], U32, name="wa_raw", align_bytes=64)
         for h in range(2):
-            g = keep.tile([P, HALF], U32, name=f"tok_g{h}", align_bytes=64)
-            nc.vector.tensor_copy(g[:], word_pool[:].indirect(offsets[:, 16 * h : 16 * (h + 1)]))
-            tok_g.append(g)
+            nc.vector.tensor_copy(tok_g[:, h * HALF : (h + 1) * HALF], word_pool[:].indirect(offsets[:, 16 * h : 16 * (h + 1)]))
 
         h_bf = []
         z_ps = []
         for c in range(I // CHUNK):
             z = psum.tile([P, PACK, CHUNK], F32, name=f"z_ps{c}")
-            h, lo = divmod(c * CHUNK, HALF)
             for t in range(PACK):
                 nc.tensor.matmul_mx(
                     out=z[:, t, :],
                     lhsT=wa_codes[:, t * P : (t + 1) * P].bitcast(FP8X4),
                     lhsT_scale=wa_scales[:, t * P : (t + 1) * P],
-                    rhs=tok_g[h][:, lo : lo + CHUNK].bitcast(FP8X4),
+                    rhs=tok_g[:, c * CHUNK : (c + 1) * CHUNK].bitcast(FP8X4),
                     rhs_scale=tok_scale_g[:, c * CHUNK : (c + 1) * CHUNK],
                     start=True,
                     stop=True,
                 )
             z_ps.append(z)
-            if c < 3:
-                hb = keep.tile([P, CHUNK, PACK], BF16, name=f"h_bf{c}", align_bytes=64)
-                h_bf.append(hb)
-                nc.scalar.activation(hb[:], z[:].rearrange("p t i -> p i t"), ACT.Relu)
+            hb = keep.tile([P, CHUNK, PACK], BF16, name=f"h_bf{c}", align_bytes=64)
+            h_bf.append(hb)
+            nc.scalar.activation(hb[:], z[:].rearrange("p t i -> p i t"), ACT.Relu, bias=xf[0][:, 0:1])
 
-        wb_bf = keep.tile([P, E, PACK], BF16, name="wb_bf", align_bytes=64)
+        wb_bf = keep.tile([P, E, PACK], BF16, name="word_pool", align_bytes=64)
         nc.vector.tensor_copy(wb_bf[:].rearrange("p (c i) j -> p c j i", i=PACK), wb_raw[:].rearrange("p j (c i) -> p c j i", i=PACK))
         wb_codes = keep.tile([P, E], U32, name="wb_codes", align_bytes=64)
         wb_scales = keep.tile([P, E], U8, name="wb_scales", align_bytes=64)
 
-        h_codes = keep.tile([P, I], U32, name="h_codes", align_bytes=64)
+        h_codes = keep.tile([P, I], U32, name="word_pool", align_bytes=64)
         h_scales = keep.tile([P, I], U8, name="h_scales", align_bytes=64)
 
         def quantise_h(c):
@@ -150,39 +140,56 @@ def tile_attend_depthffn_kernel(tc, tok_words, tok_scales, wa, wb, rw, res, offs
             )
             return o
 
-        o_half = [keep.tile([P, HALF], F32, name=f"o_sb{h}") for h in range(2)]
-        quantise_h(0)
         nc.vector.quantize_mx(out=wb_codes[:].bitcast(FP8X4), scales=wb_scales[:], in_=wb_bf[:].rearrange("p e j -> p (e j)"))
+        quantise_h(0)
         quantise_h(1)
-        nc.scalar.copy(o_half[0][:], second_layer(0, 0, HALF, "o_ps0")[:])
-        h_bf.append(keep.tile([P, CHUNK, PACK], BF16, name="h_bf1", align_bytes=64))
-        nc.vector.tensor_scalar_max(h_bf[3][:], z_ps[3][:].rearrange("p t i -> p i t"), 0.0)
         quantise_h(2)
+        x_half = [keep.tile([P, HALF], F32, name=f"x_half{h}") for h in range(2)]
+        o_first = second_layer(0, 0, HALF, "o_ps0")
+        nc.vector.tensor_tensor(x_half[0][:], o_first[:], rw_flat[:, 0:HALF], ALU.mult)
         quantise_h(3)
-        xf.append(keep.tile([P, T], F32, name="h_bf2", align_bytes=64))
-        nc.gpsimd.memset(xf[1][:], 0.0)
-        nc.scalar.copy(o_half[1][:], second_layer(0, HALF, HALF, "o_ps2")[:])
-        o_last_ps = second_layer(1, 0, I, "o_ps3")
-
-        turned = []
-        for b, (lo, hi) in enumerate(TURN_COLS):
-            acc = psum.tile([P, hi - lo], F32, name=f"z_ps{b}")
-            for k in range((hi - lo) // P):
-                nc.tensor.matmul(acc[:, k * P : (k + 1) * P], res_first[:, lo + k * P : lo + (k + 1) * P], ident[:], start=(k == 0), stop=False, is_transpose=True)
-            turned.append(acc)
-
-        def scatter_first(h):
-            nc.vector.tensor_tensor(
-                xf[0][:].indirect(offsets[:, 16 * h : 16 * (h + 1)]),
-                o_half[h][:],
-                rw_flat[:, h * HALF : (h + 1) * HALF],
-                ALU.mult,
-            )
-
-        scatter_first(0)
+        o_half = keep.tile([P, HALF], F32, name="o_half")
+        nc.scalar.copy(o_half[:], second_layer(0, HALF, HALF, "o_ps2")[:])
+        nc.gpsimd.tensor_tensor(x_half[1][:], o_half[:], rw_flat[:, HALF:I], ALU.mult)
+        o_last = keep.tile([P, I], F32, name="o_last")
+        nc.scalar.copy(o_last[:], second_layer(1, 0, I, "o_ps3")[:])
         x_last = keep.tile([P, I], F32, name="x_last")
-        nc.vector.tensor_tensor(x_last[:], o_last_ps[:], rw_flat, ALU.mult)
-        scatter_first(1)
+        nc.gpsimd.tensor_tensor(x_last[:], o_last[:], rw_flat, ALU.mult)
+
+        def turn_onto(acc, src, lo, hi, first):
+            blocks = (hi - lo) // P
+            for k in range(blocks):
+                nc.tensor.matmul(
+                    acc[:, k * P : (k + 1) * P],
+                    src[:, lo + k * P : lo + (k + 1) * P],
+                    ident[:],
+                    start=(first and k == 0),
+                    stop=(not first and k == blocks - 1),
+                    is_transpose=True,
+                )
+
+        def sum_out(acc, width, name):
+            sm = keep.tile([P, width], F32, name=name)
+            nc.scalar.copy(sm[:], acc)
+            return sm
+
+        def turn_back(sm, rows, lo, hi, bank, name):
+            back = psum.tile([P, hi - lo], F32, name=bank)
+            for k in range((hi - lo) // P):
+                nc.tensor.transpose(back[:, k * P : (k + 1) * P], sm[:, k * P : (k + 1) * P], ident[:])
+            yb = keep.tile([P, hi - lo], F32, name=name)
+            nc.scalar.copy(yb[:], back[:])
+            nc.scalar.dma_start(out[rows, lo:hi], yb[:])
+
+        two_banks = psum.tile([P, 2, I], F32, name="o_ps2")
+        third_bank = psum.tile([P, I], F32, name="o_ps3")
+        banks = [two_banks[:, 0, :], two_banks[:, 1, :], third_bank[:]]
+        turned = [banks[b][:, 0 : hi - lo] for b, (lo, hi) in enumerate(TURN_COLS)]
+        for b, (lo, hi) in enumerate(TURN_COLS):
+            turn_onto(turned[b], res_first, lo, hi, True)
+
+        for h in range(2):
+            nc.vector.tensor_copy(xf[0][:].indirect(offsets[:, 16 * h : 16 * (h + 1)]), x_half[h][:])
         nc.vector.tensor_copy(xf[1][:].indirect(offsets[:]), x_last[:])
 
         for n, (lo, hi) in enumerate(POOL_COLS):
@@ -192,23 +199,13 @@ def tile_attend_depthffn_kernel(tc, tok_words, tok_scales, wa, wb, rw, res, offs
 
         sums = []
         for b, (lo, hi) in enumerate(TURN_COLS):
-            blocks = (hi - lo) // P
-            for k in range(blocks):
-                nc.tensor.matmul(turned[b][:, k * P : (k + 1) * P], xf[0][:, lo + k * P : lo + (k + 1) * P], ident[:], start=False, stop=(k == blocks - 1), is_transpose=True)
-            sm = keep.tile([P, hi - lo], F32, name=f"sum_t{b}")
-            nc.scalar.copy(sm[:], turned[b][:])
-            sums.append(sm)
+            turn_onto(turned[b], xf[0], lo, hi, False)
+            sums.append(sum_out(turned[b], hi - lo, f"sum_t{b}"))
         for b, (lo, hi) in enumerate(TURN_COLS):
-            back = psum.tile([P, hi - lo], F32, name=f"z_ps{2 + b}")
-            for k in range((hi - lo) // P):
-                nc.tensor.transpose(back[:, k * P : (k + 1) * P], sums[b][:, k * P : (k + 1) * P], ident[:])
-            yb = keep.tile([P, hi - lo], F32, name=f"y_turn{b}")
-            nc.scalar.copy(yb[:], back[:])
-            nc.scalar.dma_start(out[0:P, lo:hi], yb[:])
+            turn_back(sums[b], slice(0, P), lo, hi, f"z_ps{1 + b}", f"y_turn{b}")
 
-        edges = [0, 128, 384, 896, 1408, 1920, 2048]
-        for n in range(len(edges) - 1):
-            cols = slice(edges[n], edges[n + 1])
-            yl = keep.tile([P, edges[n + 1] - edges[n]], F32, name=f"y_last{n}")
+        for n in range(len(LAST_EDGES) - 1):
+            cols = slice(LAST_EDGES[n], LAST_EDGES[n + 1])
+            yl = keep.tile([P, LAST_EDGES[n + 1] - LAST_EDGES[n]], F32, name=f"y_last{n}")
             nc.vector.tensor_tensor(yl[:], xf[1][:, cols], res_last[:, cols], ALU.add)
             nc.sync.dma_start(out[P:E, cols], yl[:])

@@ -22,7 +22,7 @@ HALF = 256
 CHUNK = 128
 POOL_COLS = [(0, 384), (384, 896), (896, 1152)]
 TURN_COLS = [(1152, 1408), (1408, 1792), (1792, 2048)]
-CAST_SPLIT = 48
+CAST_SPLIT = 84
 LAST_EDGES = [0, 128, 384, 896, 1408, 1920, 2048]
 
 
@@ -34,45 +34,38 @@ def tile_attend_depthffn_kernel(tc, tok_words, tok_scales, wa, wb, rw, res, offs
 
         offsets = keep.tile([P, I // 16], U16, name="offsets")
 
-        rw_cols = keep.tile([P, PACK], F32, name="rw_cols")
+        rw_cols = keep.tile([P, PACK], F32, name="wa_bf", align_bytes=64)
 
-        wa_raw = keep.tile([P, PACK, F], F32, name="wa_raw", align_bytes=64)
-        nc.sync.dma_start(wa_raw[:], wa.rearrange("(p j) f -> p j f", j=PACK))
         nc.sync.dma_start(offsets[:], offs)
-
+        nc.sync.dma_start(rw_cols[:], rw.rearrange("o (p j) -> (o p) j", j=PACK))
         scale_pool = keep.tile([P, T], U8, name="scale_pool", align_bytes=64)
         nc.gpsimd.memset(scale_pool[:].bitcast(I32), 0)
-        for r in range(4):
-            nc.sync.dma_start(
-                scale_pool[r:P:32, :].bitcast(I32),
-                tok_scales[0, r:16:4, :].bitcast(I32),
-            )
-        nc.sync.dma_start(rw_cols[:], rw.rearrange("o (p j) -> (o p) j", j=PACK))
+        wa_raw = keep.tile([P, PACK, F], F32, name="wa_raw", align_bytes=64)
+        wa_rows = wa.rearrange("(p j) f -> p j f", j=PACK)
+        nc.sync.dma_start(wa_raw[:, 0:1, :], wa_rows[:, 0:1, :])
+        nc.sync.dma_start(scale_pool[0:P:8, :].bitcast(I32), tok_scales[0].bitcast(I32))
+        nc.sync.dma_start(wa_raw[:, 1:PACK, :], wa_rows[:, 1:PACK, :])
         word_pool = keep.tile([P, T], U32, name="word_pool", align_bytes=64)
         nc.sync.dma_start(
             word_pool[:].bitcast(I32),
             tok_words[0].rearrange("p t r -> p (t r)").bitcast(I32),
         )
-        wb_raw = keep.tile([P, PACK, E], F32, name="wb_raw")
+
+        scale_g = keep.tile([P, I], U8, name="scale_g", align_bytes=64)
+        nc.vector.tensor_copy(scale_g[:], scale_pool[:].indirect(offsets[:]))
+        tok_scale_g = keep.tile([P, I], U8, name="tok_scale_g", align_bytes=64)
+        nc.gpsimd.memset(tok_scale_g[:].bitcast(I32), 0)
+        for r in range(4):
+            nc.sync.dma_start(tok_scale_g[r:P:32, :].bitcast(I32), scale_g[8 * r : P : 32, :].bitcast(I32))
+        wb_raw = keep.tile([P, PACK, E], F32, name="scale_pool", align_bytes=64)
         nc.sync.dma_start(wb_raw[:], wb.rearrange("(p j) e -> p j e", j=PACK))
-        res_first = keep.tile([P, T], F32, name="res_first")
-        res_last = keep.tile([P, T], F32, name="res_last")
-        nc.sync.dma_start(res_first[:], res[0:P, :])
-        nc.sync.dma_start(res_last[:], res[P:E, :])
 
         xf = [keep.tile([P, T], F32, name=f"xf{g}") for g in range(2)]
         ident = keep.tile([P, P], F32, name="ident")
         nc.vector.memset(ident[:], 0.0)
         nc.vector.memset(xf[0][:], 0.0)
-        nc.vector.memset(xf[1][:, 0 : T // 2], 0.0)
         make_identity(nc, ident[:], nomemset=True)
-        nc.gpsimd.memset(xf[1][:, T // 2 : T], 0.0)
-
-        wa_src = wa_raw[:].rearrange("p j (m t) -> p m j t", t=PACK)
-        wa_bf = keep.tile([P, PACK, P, PACK], BF16, name="wa_bf", align_bytes=64)
-        wa_dst = wa_bf[:].rearrange("p t m j -> p m j t")
-        nc.vector.tensor_copy(wa_dst[:, 0:CAST_SPLIT], wa_src[:, 0:CAST_SPLIT])
-        nc.scalar.copy(wa_dst[:, CAST_SPLIT:P], wa_src[:, CAST_SPLIT:P])
+        nc.gpsimd.memset(xf[1][:], 0.0)
 
         rw_ps = psum.tile([P, PACK, P], F32, name="o_ps0")
         for j in range(PACK):
@@ -81,12 +74,20 @@ def tile_attend_depthffn_kernel(tc, tok_words, tok_scales, wa, wb, rw, res, offs
         nc.scalar.copy(rw_rows[:], rw_ps[:].rearrange("p j n -> p n j"))
         rw_flat = rw_rows[:].rearrange("p n j -> p (n j)")
 
-        tok_scale_g = keep.tile([P, I], U8, name="tok_scale_g", align_bytes=64)
-        nc.vector.tensor_copy(tok_scale_g[:], scale_pool[:].indirect(offsets[:]))
+        wa_src = wa_raw[:].rearrange("p j (m t) -> p m j t", t=PACK)
+        wa_bf = keep.tile([P, PACK, P, PACK], BF16, name="wa_bf", align_bytes=64)
+        wa_dst = wa_bf[:].rearrange("p t m j -> p m j t")
+        nc.vector.tensor_copy(wa_dst[:, 0:CAST_SPLIT], wa_src[:, 0:CAST_SPLIT])
+        nc.scalar.copy(wa_dst[:, CAST_SPLIT:P], wa_src[:, CAST_SPLIT:P])
 
         wa_codes = keep.tile([P, F], U32, name="wa_codes", align_bytes=64)
-        wa_scales = keep.tile([P, F], U8, name="scale_pool", align_bytes=64)
+        wa_scales = keep.tile([P, F], U8, name="wa_scales", align_bytes=64)
         nc.vector.quantize_mx(out=wa_codes[:].bitcast(FP8X4), scales=wa_scales[:], in_=wa_bf[:].rearrange("p t m j -> p (t m j)"))
+
+        res_first = keep.tile([P, T], F32, name="wa_bf", align_bytes=64)
+        nc.sync.dma_start(res_first[:], res[0:P, :])
+        res_last = keep.tile([P, T], F32, name="scale_g", align_bytes=64)
+        nc.sync.dma_start(res_last[:], res[P:E, :])
 
         tok_g = keep.tile([P, I], U32, name="wa_raw", align_bytes=64)
         for h in range(2):
@@ -111,12 +112,20 @@ def tile_attend_depthffn_kernel(tc, tok_words, tok_scales, wa, wb, rw, res, offs
             h_bf.append(hb)
             nc.scalar.activation(hb[:], z[:].rearrange("p t i -> p i t"), ACT.Relu, bias=xf[0][:, 0:1])
 
-        wb_bf = keep.tile([P, E, PACK], BF16, name="word_pool", align_bytes=64)
-        nc.vector.tensor_copy(wb_bf[:].rearrange("p (c i) j -> p c j i", i=PACK), wb_raw[:].rearrange("p j (c i) -> p c j i", i=PACK))
         wb_codes = keep.tile([P, E], U32, name="wb_codes", align_bytes=64)
         wb_scales = keep.tile([P, E], U8, name="wb_scales", align_bytes=64)
+        wb_src = wb_raw[:].rearrange("p j (c i) -> p c j i", i=PACK)
+        wb_bf = keep.tile([P, E, PACK], BF16, name="word_pool", align_bytes=64)
 
-        h_codes = keep.tile([P, I], U32, name="word_pool", align_bytes=64)
+        def cast_wb(g):
+            dst = wb_bf[:, g * P : (g + 1) * P, :].rearrange("p (c i) j -> p c j i", i=PACK)
+            nc.vector.tensor_copy(dst, wb_src[:, 32 * g : 32 * (g + 1)])
+
+        def quantise_wb(g):
+            cols = slice(g * P, (g + 1) * P)
+            nc.vector.quantize_mx(out=wb_codes[:, cols].bitcast(FP8X4), scales=wb_scales[:, cols], in_=wb_bf[:, cols, :].rearrange("p e j -> p (e j)"))
+
+        h_codes = keep.tile([P, I], U32, name="h_codes", align_bytes=64)
         h_scales = keep.tile([P, I], U8, name="h_scales", align_bytes=64)
 
         def quantise_h(c):
@@ -140,7 +149,10 @@ def tile_attend_depthffn_kernel(tc, tok_words, tok_scales, wa, wb, rw, res, offs
             )
             return o
 
-        nc.vector.quantize_mx(out=wb_codes[:].bitcast(FP8X4), scales=wb_scales[:], in_=wb_bf[:].rearrange("p e j -> p (e j)"))
+        cast_wb(0)
+        cast_wb(1)
+        quantise_wb(0)
+        quantise_wb(1)
         quantise_h(0)
         quantise_h(1)
         quantise_h(2)

@@ -20,10 +20,10 @@ P = 128
 PACK = 4
 HALF = 256
 CHUNK = 128
-POOL_COLS = [(0, 384), (384, 896), (896, 1152)]
+POOL_COLS = [(0, 256), (256, 576), (576, 896), (896, 1152)]
 TURN_COLS = [(1152, 1408), (1408, 1792), (1792, 2048)]
 CAST_SPLIT = 84
-LAST_EDGES = [0, 128, 384, 896, 1408, 1920, 2048]
+LAST_EDGES = [0, 512, 1024, 1536, 2048]
 
 
 def tile_attend_depthffn_kernel(tc, tok_words, tok_scales, wa, wb, rw, res, offs, out):
@@ -36,13 +36,13 @@ def tile_attend_depthffn_kernel(tc, tok_words, tok_scales, wa, wb, rw, res, offs
 
         rw_cols = keep.tile([P, PACK], F32, name="wa_bf", align_bytes=64)
 
-        nc.sync.dma_start(offsets[:], offs)
-        nc.sync.dma_start(rw_cols[:], rw.rearrange("o (p j) -> (o p) j", j=PACK))
         scale_pool = keep.tile([P, T], U8, name="scale_pool", align_bytes=64)
         nc.gpsimd.memset(scale_pool[:].bitcast(I32), 0)
         wa_raw = keep.tile([P, PACK, F], F32, name="wa_raw", align_bytes=64)
         wa_rows = wa.rearrange("(p j) f -> p j f", j=PACK)
         nc.sync.dma_start(wa_raw[:, 0:1, :], wa_rows[:, 0:1, :])
+        nc.sync.dma_start(offsets[:], offs)
+        nc.sync.dma_start(rw_cols[:], rw.rearrange("o (p j) -> (o p) j", j=PACK))
         nc.sync.dma_start(scale_pool[0:P:8, :].bitcast(I32), tok_scales[0].bitcast(I32))
         nc.sync.dma_start(wa_raw[:, 1:PACK, :], wa_rows[:, 1:PACK, :])
         word_pool = keep.tile([P, T], U32, name="word_pool", align_bytes=64)
@@ -64,8 +64,9 @@ def tile_attend_depthffn_kernel(tc, tok_words, tok_scales, wa, wb, rw, res, offs
         ident = keep.tile([P, P], F32, name="ident")
         nc.vector.memset(ident[:], 0.0)
         nc.vector.memset(xf[0][:], 0.0)
+        nc.vector.memset(xf[1][:, 0 : T // 2], 0.0)
         make_identity(nc, ident[:], nomemset=True)
-        nc.gpsimd.memset(xf[1][:], 0.0)
+        nc.gpsimd.memset(xf[1][:, T // 2 : T], 0.0)
 
         rw_ps = psum.tile([P, PACK, P], F32, name="o_ps0")
         for j in range(PACK):
@@ -86,8 +87,6 @@ def tile_attend_depthffn_kernel(tc, tok_words, tok_scales, wa, wb, rw, res, offs
 
         res_first = keep.tile([P, T], F32, name="wa_bf", align_bytes=64)
         nc.sync.dma_start(res_first[:], res[0:P, :])
-        res_last = keep.tile([P, T], F32, name="scale_g", align_bytes=64)
-        nc.sync.dma_start(res_last[:], res[P:E, :])
 
         tok_g = keep.tile([P, I], U32, name="wa_raw", align_bytes=64)
         for h in range(2):
@@ -151,6 +150,8 @@ def tile_attend_depthffn_kernel(tc, tok_words, tok_scales, wa, wb, rw, res, offs
 
         cast_wb(0)
         cast_wb(1)
+        res_last = keep.tile([P, T], F32, name="scale_pool", align_bytes=64)
+        nc.sync.dma_start(res_last[:], res[P:E, :])
         quantise_wb(0)
         quantise_wb(1)
         quantise_h(0)
@@ -213,8 +214,9 @@ def tile_attend_depthffn_kernel(tc, tok_words, tok_scales, wa, wb, rw, res, offs
         for b, (lo, hi) in enumerate(TURN_COLS):
             turn_onto(turned[b], xf[0], lo, hi, False)
             sums.append(sum_out(turned[b], hi - lo, f"sum_t{b}"))
-        for b, (lo, hi) in enumerate(TURN_COLS):
-            turn_back(sums[b], slice(0, P), lo, hi, f"z_ps{1 + b}", f"y_turn{b}")
+            if b > 0:
+                turn_back(sums[b - 1], slice(0, P), *TURN_COLS[b - 1], f"z_ps{b}", f"y_turn{b - 1}")
+        turn_back(sums[-1], slice(0, P), *TURN_COLS[-1], "z_ps3", "y_turn2")
 
         for n in range(len(LAST_EDGES) - 1):
             cols = slice(LAST_EDGES[n], LAST_EDGES[n + 1])

@@ -23,7 +23,7 @@ CHUNK = 128
 POOL_COLS = [(0, 256), (256, 576), (576, 896), (896, 1152)]
 TURN_COLS = [(1152, 1408), (1408, 1792), (1792, 2048)]
 CAST_SPLIT = 84
-LAST_EDGES = [0, 512, 1024, 1536, 2048]
+LAST_EDGES = [0, 512, 1280, 2048]
 
 
 def tile_attend_depthffn_kernel(tc, tok_words, tok_scales, wa, wb, rw, res, offs, out):
@@ -161,9 +161,11 @@ def tile_attend_depthffn_kernel(tc, tok_words, tok_scales, wa, wb, rw, res, offs
         o_first = second_layer(0, 0, HALF, "o_ps0")
         nc.vector.tensor_tensor(x_half[0][:], o_first[:], rw_flat[:, 0:HALF], ALU.mult)
         quantise_h(3)
-        o_half = keep.tile([P, HALF], F32, name="o_half")
-        nc.scalar.copy(o_half[:], second_layer(0, HALF, HALF, "o_ps2")[:])
-        nc.gpsimd.tensor_tensor(x_half[1][:], o_half[:], rw_flat[:, HALF:I], ALU.mult)
+        for c, bank in ((2, "z_ps0"), (3, "o_ps2")):
+            o_chunk = keep.tile([P, CHUNK], F32, name=f"o_chunk{c}")
+            nc.scalar.copy(o_chunk[:], second_layer(0, c * CHUNK, CHUNK, bank)[:])
+            dst = x_half[1][:, (c - 2) * CHUNK : (c - 1) * CHUNK]
+            nc.gpsimd.tensor_tensor(dst, o_chunk[:], rw_flat[:, c * CHUNK : (c + 1) * CHUNK], ALU.mult)
         o_last = keep.tile([P, I], F32, name="o_last")
         nc.scalar.copy(o_last[:], second_layer(1, 0, I, "o_ps3")[:])
         x_last = keep.tile([P, I], F32, name="x_last")
@@ -205,10 +207,10 @@ def tile_attend_depthffn_kernel(tc, tok_words, tok_scales, wa, wb, rw, res, offs
             nc.vector.tensor_copy(xf[0][:].indirect(offsets[:, 16 * h : 16 * (h + 1)]), x_half[h][:])
         nc.vector.tensor_copy(xf[1][:].indirect(offsets[:]), x_last[:])
 
-        for n, (lo, hi) in enumerate(POOL_COLS):
-            y = keep.tile([P, hi - lo], F32, name=f"y_pool{n}")
-            nc.gpsimd.tensor_tensor(y[:], xf[0][:, lo:hi], res_first[:, lo:hi], ALU.add)
-            nc.sync.dma_start(out[0:P, lo:hi], y[:])
+        y_pool = keep.tile([P, POOL_COLS[-1][1]], F32, name="o_last")
+        for lo, hi in POOL_COLS:
+            nc.gpsimd.tensor_tensor(y_pool[:, lo:hi], xf[0][:, lo:hi], res_first[:, lo:hi], ALU.add)
+            nc.sync.dma_start(out[0:P, lo:hi], y_pool[:, lo:hi])
 
         sums = []
         for b, (lo, hi) in enumerate(TURN_COLS):

@@ -60,13 +60,11 @@ def tile_attend_depthffn_kernel(tc, tok_words, tok_scales, wa, wb, rw, res, offs
         wb_raw = keep.tile([P, PACK, E], F32, name="scale_pool", align_bytes=64)
         nc.sync.dma_start(wb_raw[:], wb.rearrange("(p j) e -> p j e", j=PACK))
 
-        xf = [keep.tile([P, T], F32, name=f"xf{g}") for g in range(2)]
+        xf = [keep.tile([P, T], F32, name="xf0")]
         ident = keep.tile([P, P], F32, name="ident")
         nc.vector.memset(ident[:], 0.0)
         nc.vector.memset(xf[0][:], 0.0)
-        nc.vector.memset(xf[1][:, 0 : T // 2], 0.0)
         make_identity(nc, ident[:], nomemset=True)
-        nc.gpsimd.memset(xf[1][:, T // 2 : T], 0.0)
 
         rw_ps = psum.tile([P, PACK, P], F32, name="o_ps0")
         for j in range(PACK):
@@ -85,7 +83,9 @@ def tile_attend_depthffn_kernel(tc, tok_words, tok_scales, wa, wb, rw, res, offs
         wa_scales = keep.tile([P, F], U8, name="wa_scales", align_bytes=64)
         nc.vector.quantize_mx(out=wa_codes[:].bitcast(FP8X4), scales=wa_scales[:], in_=wa_bf[:].rearrange("p t m j -> p (t m j)"))
 
-        res_first = keep.tile([P, T], F32, name="wa_bf", align_bytes=64)
+        xf.append(keep.tile([P, T], F32, name="wa_bf", align_bytes=64))
+        nc.gpsimd.memset(xf[1][:], 0.0)
+        res_first = keep.tile([P, T], F32, name="scale_g", align_bytes=64)
         nc.sync.dma_start(res_first[:], res[0:P, :])
 
         tok_g = keep.tile([P, I], U32, name="wa_raw", align_bytes=64)

@@ -18,12 +18,13 @@ ALU = mybir.AluOpType
 
 P = 128
 PACK = 4
-HALF = 256
+HALF = I // 2
 CHUNK = 128
+LIST_COLS = HALF // 16
+
 POOL_COLS = [(0, 256), (256, 576), (576, 896), (896, 1152)]
 TURN_COLS = [(1152, 1408), (1408, 1792), (1792, 2048)]
-CAST_SPLIT = 84
-LAST_EDGES = [0, 512, 1280, 2048]
+LAST_COLS = [(0, 512), (512, 1280), (1280, 2048)]
 
 
 def tile_attend_depthffn_kernel(tc, tok_words, tok_scales, wa, wb, rw, res, offs, out):
@@ -33,40 +34,39 @@ def tile_attend_depthffn_kernel(tc, tok_words, tok_scales, wa, wb, rw, res, offs
         psum = ctx.enter_context(tc.psum_pool(name="psum", bufs=1))
 
         offsets = keep.tile([P, I // 16], U16, name="offsets")
+        rw_cols = keep.tile([P, PACK], F32, name="rw_cols", tag="cast_s", align_bytes=64)
 
-        rw_cols = keep.tile([P, PACK], F32, name="wa_bf", align_bytes=64)
-
-        scale_pool = keep.tile([P, T], U8, name="scale_pool", align_bytes=64)
+        scale_pool = keep.tile([P, T], U8, name="scale_pool", tag="scales", align_bytes=64)
         nc.gpsimd.memset(scale_pool[:].bitcast(I32), 0)
-        wa_raw = keep.tile([P, PACK, F], F32, name="wa_raw", align_bytes=64)
+        wa_raw = keep.tile([P, PACK, F], F32, name="wa_raw", tag="wa", align_bytes=64)
         wa_rows = wa.rearrange("(p j) f -> p j f", j=PACK)
         nc.sync.dma_start(wa_raw[:, 0:1, :], wa_rows[:, 0:1, :])
         nc.sync.dma_start(offsets[:], offs)
         nc.sync.dma_start(rw_cols[:], rw.rearrange("o (p j) -> (o p) j", j=PACK))
         nc.sync.dma_start(scale_pool[0:P:8, :].bitcast(I32), tok_scales[0].bitcast(I32))
         nc.sync.dma_start(wa_raw[:, 1:PACK, :], wa_rows[:, 1:PACK, :])
-        word_pool = keep.tile([P, T], U32, name="word_pool", align_bytes=64)
+        word_pool = keep.tile([P, T], U32, name="word_pool", tag="words", align_bytes=64)
         nc.sync.dma_start(
             word_pool[:].bitcast(I32),
             tok_words[0].rearrange("p t r -> p (t r)").bitcast(I32),
         )
 
-        scale_g = keep.tile([P, I], U8, name="scale_g", align_bytes=64)
+        scale_g = keep.tile([P, I], U8, name="scale_g", tag="gathered", align_bytes=64)
         nc.vector.tensor_copy(scale_g[:], scale_pool[:].indirect(offsets[:]))
-        tok_scale_g = keep.tile([P, I], U8, name="tok_scale_g", align_bytes=64)
-        nc.gpsimd.memset(tok_scale_g[:].bitcast(I32), 0)
+        tok_plane = keep.tile([P, I], U8, name="tok_plane", align_bytes=64)
+        nc.gpsimd.memset(tok_plane[:].bitcast(I32), 0)
         for r in range(4):
-            nc.sync.dma_start(tok_scale_g[r:P:32, :].bitcast(I32), scale_g[8 * r : P : 32, :].bitcast(I32))
-        wb_raw = keep.tile([P, PACK, E], F32, name="scale_pool", align_bytes=64)
+            nc.sync.dma_start(tok_plane[r:P:32, :].bitcast(I32), scale_g[8 * r : P : 32, :].bitcast(I32))
+        wb_raw = keep.tile([P, PACK, E], F32, name="wb_raw", tag="scales", align_bytes=64)
         nc.sync.dma_start(wb_raw[:], wb.rearrange("(p j) e -> p j e", j=PACK))
 
-        xf = [keep.tile([P, T], F32, name="xf0")]
+        xf_first = keep.tile([P, T], F32, name="xf_first")
         ident = keep.tile([P, P], F32, name="ident")
         nc.vector.memset(ident[:], 0.0)
-        nc.vector.memset(xf[0][:], 0.0)
+        nc.vector.memset(xf_first[:], 0.0)
         make_identity(nc, ident[:], nomemset=True)
 
-        rw_ps = psum.tile([P, PACK, P], F32, name="o_ps0")
+        rw_ps = psum.tile([P, PACK, P], F32, name="rw_ps", tag="bank_a")
         for j in range(PACK):
             nc.tensor.transpose(rw_ps[:, j, :], rw_cols[:, j : j + 1].to_broadcast([P, P]), ident[:])
         rw_rows = keep.tile([P, P, PACK], F32, name="rw_rows")
@@ -74,58 +74,68 @@ def tile_attend_depthffn_kernel(tc, tok_words, tok_scales, wa, wb, rw, res, offs
         rw_flat = rw_rows[:].rearrange("p n j -> p (n j)")
 
         wa_src = wa_raw[:].rearrange("p j (m t) -> p m j t", t=PACK)
-        wa_bf = keep.tile([P, PACK, P, PACK], BF16, name="wa_bf", align_bytes=64)
-        wa_dst = wa_bf[:].rearrange("p t m j -> p m j t")
-        nc.vector.tensor_copy(wa_dst[:, 0:CAST_SPLIT], wa_src[:, 0:CAST_SPLIT])
-        nc.scalar.copy(wa_dst[:, CAST_SPLIT:P], wa_src[:, CAST_SPLIT:P])
+        wa_bf = [keep.tile([P, 2, P, PACK], BF16, name=f"wa_bf{u}", tag=tag, align_bytes=64) for u, tag in enumerate(("cast_v", "cast_s"))]
+        nc.vector.tensor_copy(wa_bf[0][:].rearrange("p t m j -> p m j t"), wa_src[:, :, :, 0:2])
+        nc.scalar.copy(wa_bf[1][:].rearrange("p t m j -> p m j t"), wa_src[:, :, :, 2:4])
 
         wa_codes = keep.tile([P, F], U32, name="wa_codes", align_bytes=64)
         wa_scales = keep.tile([P, F], U8, name="wa_scales", align_bytes=64)
-        nc.vector.quantize_mx(out=wa_codes[:].bitcast(FP8X4), scales=wa_scales[:], in_=wa_bf[:].rearrange("p t m j -> p (t m j)"))
+        for u in range(2):
+            cols = slice(2 * P * u, 2 * P * (u + 1))
+            nc.vector.quantize_mx(
+                out=wa_codes[:, cols].bitcast(FP8X4),
+                scales=wa_scales[:, cols],
+                in_=wa_bf[u][:].rearrange("p t m j -> p (t m j)"),
+            )
 
-        xf.append(keep.tile([P, T], F32, name="wa_bf", align_bytes=64))
-        nc.gpsimd.memset(xf[1][:], 0.0)
-        res_first = keep.tile([P, T], F32, name="scale_g", align_bytes=64)
+        xf_last = keep.tile([P, T], F32, name="xf_last", tag="cast_s", align_bytes=64)
+        nc.gpsimd.memset(xf_last[:], 0.0)
+        res_first = keep.tile([P, T], F32, name="res_first", tag="gathered", align_bytes=64)
         nc.sync.dma_start(res_first[:], res[0:P, :])
 
-        tok_g = keep.tile([P, I], U32, name="wa_raw", align_bytes=64)
+        tok_g = keep.tile([P, I], U32, name="tok_g", tag="wa", align_bytes=64)
         for h in range(2):
-            nc.vector.tensor_copy(tok_g[:, h * HALF : (h + 1) * HALF], word_pool[:].indirect(offsets[:, 16 * h : 16 * (h + 1)]))
+            nc.vector.tensor_copy(
+                tok_g[:, h * HALF : (h + 1) * HALF],
+                word_pool[:].indirect(offsets[:, h * LIST_COLS : (h + 1) * LIST_COLS]),
+            )
 
         h_bf = []
-        z_ps = []
         for c in range(I // CHUNK):
-            z = psum.tile([P, PACK, CHUNK], F32, name=f"z_ps{c}")
+            z = psum.tile([P, PACK, CHUNK], F32, name=f"z{c}", tag=f"bank_z{c}")
             for t in range(PACK):
                 nc.tensor.matmul_mx(
                     out=z[:, t, :],
                     lhsT=wa_codes[:, t * P : (t + 1) * P].bitcast(FP8X4),
                     lhsT_scale=wa_scales[:, t * P : (t + 1) * P],
                     rhs=tok_g[:, c * CHUNK : (c + 1) * CHUNK].bitcast(FP8X4),
-                    rhs_scale=tok_scale_g[:, c * CHUNK : (c + 1) * CHUNK],
+                    rhs_scale=tok_plane[:, c * CHUNK : (c + 1) * CHUNK],
                     start=True,
                     stop=True,
                 )
-            z_ps.append(z)
             hb = keep.tile([P, CHUNK, PACK], BF16, name=f"h_bf{c}", align_bytes=64)
             h_bf.append(hb)
-            nc.scalar.activation(hb[:], z[:].rearrange("p t i -> p i t"), ACT.Relu, bias=xf[0][:, 0:1])
+            nc.scalar.activation(hb[:], z[:].rearrange("p t i -> p i t"), ACT.Relu, bias=xf_first[:, 0:1])
 
         wb_codes = keep.tile([P, E], U32, name="wb_codes", align_bytes=64)
         wb_scales = keep.tile([P, E], U8, name="wb_scales", align_bytes=64)
         wb_src = wb_raw[:].rearrange("p j (c i) -> p c j i", i=PACK)
-        wb_bf = keep.tile([P, E, PACK], BF16, name="word_pool", align_bytes=64)
-
-        def cast_wb(g):
-            dst = wb_bf[:, g * P : (g + 1) * P, :].rearrange("p (c i) j -> p c j i", i=PACK)
-            nc.vector.tensor_copy(dst, wb_src[:, 32 * g : 32 * (g + 1)])
-
-        def quantise_wb(g):
-            cols = slice(g * P, (g + 1) * P)
-            nc.vector.quantize_mx(out=wb_codes[:, cols].bitcast(FP8X4), scales=wb_scales[:, cols], in_=wb_bf[:, cols, :].rearrange("p e j -> p (e j)"))
-
+        wb_bf = keep.tile([P, E, PACK], BF16, name="wb_bf", tag="words", align_bytes=64)
         h_codes = keep.tile([P, I], U32, name="h_codes", align_bytes=64)
         h_scales = keep.tile([P, I], U8, name="h_scales", align_bytes=64)
+        quads = P // PACK
+        for g in range(2):
+            dst = wb_bf[:, g * P : (g + 1) * P, :].rearrange("p (c i) j -> p c j i", i=PACK)
+            nc.vector.tensor_copy(dst, wb_src[:, quads * g : quads * (g + 1)])
+        res_last = keep.tile([P, T], F32, name="res_last", tag="scales", align_bytes=64)
+        nc.sync.dma_start(res_last[:], res[P:E, :])
+        for g in range(2):
+            cols = slice(g * P, (g + 1) * P)
+            nc.vector.quantize_mx(
+                out=wb_codes[:, cols].bitcast(FP8X4),
+                scales=wb_scales[:, cols],
+                in_=wb_bf[:, cols, :].rearrange("p e j -> p (e j)"),
+            )
 
         def quantise_h(c):
             cols = slice(c * CHUNK, (c + 1) * CHUNK)
@@ -136,7 +146,7 @@ def tile_attend_depthffn_kernel(tc, tok_words, tok_scales, wa, wb, rw, res, offs
             )
 
         def second_layer(g, lo, width, bank):
-            o = psum.tile([P, width], F32, name=bank)
+            o = psum.tile([P, width], F32, name=f"o{g}_{lo}", tag=bank)
             nc.tensor.matmul_mx(
                 out=o[:],
                 lhsT=wb_codes[:, g * P : (g + 1) * P].bitcast(FP8X4),
@@ -148,80 +158,70 @@ def tile_attend_depthffn_kernel(tc, tok_words, tok_scales, wa, wb, rw, res, offs
             )
             return o
 
-        cast_wb(0)
-        cast_wb(1)
-        res_last = keep.tile([P, T], F32, name="scale_pool", align_bytes=64)
-        nc.sync.dma_start(res_last[:], res[P:E, :])
-        quantise_wb(0)
-        quantise_wb(1)
-        quantise_h(0)
-        quantise_h(1)
-        quantise_h(2)
+        for c in range(3):
+            quantise_h(c)
         x_half = [keep.tile([P, HALF], F32, name=f"x_half{h}") for h in range(2)]
-        o_first = second_layer(0, 0, HALF, "o_ps0")
+        o_first = second_layer(0, 0, HALF, "bank_a")
         nc.vector.tensor_tensor(x_half[0][:], o_first[:], rw_flat[:, 0:HALF], ALU.mult)
         quantise_h(3)
-        for c, bank in ((2, "z_ps0"), (3, "o_ps2")):
+        for c, bank in ((2, "bank_z0"), (3, "banks_b")):
             o_chunk = keep.tile([P, CHUNK], F32, name=f"o_chunk{c}")
             nc.scalar.copy(o_chunk[:], second_layer(0, c * CHUNK, CHUNK, bank)[:])
-            dst = x_half[1][:, (c - 2) * CHUNK : (c - 1) * CHUNK]
+            dst = x_half[1][:, c * CHUNK - HALF : (c + 1) * CHUNK - HALF]
             nc.gpsimd.tensor_tensor(dst, o_chunk[:], rw_flat[:, c * CHUNK : (c + 1) * CHUNK], ALU.mult)
-        o_last = keep.tile([P, I], F32, name="o_last")
-        nc.scalar.copy(o_last[:], second_layer(1, 0, I, "o_ps3")[:])
+        o_last = keep.tile([P, I], F32, name="o_last", tag="pool_io")
+        nc.scalar.copy(o_last[:], second_layer(1, 0, I, "bank_c")[:])
         x_last = keep.tile([P, I], F32, name="x_last")
         nc.gpsimd.tensor_tensor(x_last[:], o_last[:], rw_flat, ALU.mult)
 
-        def turn_onto(acc, src, lo, hi, first):
+        def turn_onto(acc, src, lo, hi, opens):
             blocks = (hi - lo) // P
             for k in range(blocks):
                 nc.tensor.matmul(
                     acc[:, k * P : (k + 1) * P],
                     src[:, lo + k * P : lo + (k + 1) * P],
                     ident[:],
-                    start=(first and k == 0),
-                    stop=(not first and k == blocks - 1),
+                    start=(opens and k == 0),
+                    stop=(not opens and k == blocks - 1),
                     is_transpose=True,
                 )
 
-        def sum_out(acc, width, name):
-            sm = keep.tile([P, width], F32, name=name)
-            nc.scalar.copy(sm[:], acc)
-            return sm
-
-        def turn_back(sm, rows, lo, hi, bank, name):
-            back = psum.tile([P, hi - lo], F32, name=bank)
+        def turn_back(b, turned_sum):
+            lo, hi = TURN_COLS[b]
+            back = psum.tile([P, hi - lo], F32, name=f"back{b}", tag=f"bank_z{b + 1}")
             for k in range((hi - lo) // P):
-                nc.tensor.transpose(back[:, k * P : (k + 1) * P], sm[:, k * P : (k + 1) * P], ident[:])
-            yb = keep.tile([P, hi - lo], F32, name=name)
-            nc.scalar.copy(yb[:], back[:])
-            nc.scalar.dma_start(out[rows, lo:hi], yb[:])
+                nc.tensor.transpose(back[:, k * P : (k + 1) * P], turned_sum[:, k * P : (k + 1) * P], ident[:])
+            y_turn = keep.tile([P, hi - lo], F32, name=f"y_turn{b}")
+            nc.scalar.copy(y_turn[:], back[:])
+            nc.scalar.dma_start(out[0:P, lo:hi], y_turn[:])
 
-        two_banks = psum.tile([P, 2, I], F32, name="o_ps2")
-        third_bank = psum.tile([P, I], F32, name="o_ps3")
+        two_banks = psum.tile([P, 2, I], F32, name="two_banks", tag="banks_b")
+        third_bank = psum.tile([P, I], F32, name="third_bank", tag="bank_c")
         banks = [two_banks[:, 0, :], two_banks[:, 1, :], third_bank[:]]
         turned = [banks[b][:, 0 : hi - lo] for b, (lo, hi) in enumerate(TURN_COLS)]
         for b, (lo, hi) in enumerate(TURN_COLS):
             turn_onto(turned[b], res_first, lo, hi, True)
 
         for h in range(2):
-            nc.vector.tensor_copy(xf[0][:].indirect(offsets[:, 16 * h : 16 * (h + 1)]), x_half[h][:])
-        nc.vector.tensor_copy(xf[1][:].indirect(offsets[:]), x_last[:])
+            nc.vector.tensor_copy(xf_first[:].indirect(offsets[:, h * LIST_COLS : (h + 1) * LIST_COLS]), x_half[h][:])
+        nc.vector.tensor_copy(xf_last[:].indirect(offsets[:]), x_last[:])
 
-        y_pool = keep.tile([P, POOL_COLS[-1][1]], F32, name="o_last")
+        y_pool = keep.tile([P, POOL_COLS[-1][1]], F32, name="y_pool", tag="pool_io")
         for lo, hi in POOL_COLS:
-            nc.gpsimd.tensor_tensor(y_pool[:, lo:hi], xf[0][:, lo:hi], res_first[:, lo:hi], ALU.add)
+            nc.gpsimd.tensor_tensor(y_pool[:, lo:hi], xf_first[:, lo:hi], res_first[:, lo:hi], ALU.add)
             nc.sync.dma_start(out[0:P, lo:hi], y_pool[:, lo:hi])
 
         sums = []
         for b, (lo, hi) in enumerate(TURN_COLS):
-            turn_onto(turned[b], xf[0], lo, hi, False)
-            sums.append(sum_out(turned[b], hi - lo, f"sum_t{b}"))
+            turn_onto(turned[b], xf_first, lo, hi, False)
+            turned_sum = keep.tile([P, hi - lo], F32, name=f"turned_sum{b}")
+            nc.scalar.copy(turned_sum[:], turned[b])
+            sums.append(turned_sum)
             if b > 0:
-                turn_back(sums[b - 1], slice(0, P), *TURN_COLS[b - 1], f"z_ps{b}", f"y_turn{b - 1}")
-        turn_back(sums[-1], slice(0, P), *TURN_COLS[-1], "z_ps3", "y_turn2")
+                turn_back(b - 1, sums[b - 1])
+        turn_back(len(TURN_COLS) - 1, sums[-1])
 
-        for n in range(len(LAST_EDGES) - 1):
-            cols = slice(LAST_EDGES[n], LAST_EDGES[n + 1])
-            yl = keep.tile([P, LAST_EDGES[n + 1] - LAST_EDGES[n]], F32, name=f"y_last{n}")
-            nc.vector.tensor_tensor(yl[:], xf[1][:, cols], res_last[:, cols], ALU.add)
-            nc.sync.dma_start(out[P:E, cols], yl[:])
+        for n, (lo, hi) in enumerate(LAST_COLS):
+            y_last = keep.tile([P, hi - lo], F32, name=f"y_last{n}")
+            nc.vector.tensor_tensor(y_last[:], xf_last[:, lo:hi], res_last[:, lo:hi], ALU.add)
+            nc.sync.dma_start(out[P:E, lo:hi], y_last[:])

@@ -24,7 +24,7 @@ LIST_COLS = HALF // 16
 
 POOL_COLS = [(0, 256), (256, 576), (576, 896), (896, 1152)]
 TURN_COLS = [(1152, 1408), (1408, 1792), (1792, 2048)]
-LAST_COLS = [(0, 512), (512, 1280), (1280, 2048)]
+LAST_COLS = [(0, 384), (384, 896), (896, 1472), (1472, 2048)]
 
 
 def tile_attend_depthffn_kernel(tc, tok_words, tok_scales, wa, wb, rw, res, offs, out):
@@ -74,19 +74,23 @@ def tile_attend_depthffn_kernel(tc, tok_words, tok_scales, wa, wb, rw, res, offs
         rw_flat = rw_rows[:].rearrange("p n j -> p (n j)")
 
         wa_src = wa_raw[:].rearrange("p j (m t) -> p m j t", t=PACK)
-        wa_bf = [keep.tile([P, 2, P, PACK], BF16, name=f"wa_bf{u}", tag=tag, align_bytes=64) for u, tag in enumerate(("cast_v", "cast_s"))]
-        nc.vector.tensor_copy(wa_bf[0][:].rearrange("p t m j -> p m j t"), wa_src[:, :, :, 0:2])
-        nc.scalar.copy(wa_bf[1][:].rearrange("p t m j -> p m j t"), wa_src[:, :, :, 2:4])
+        wa_low = keep.tile([P, 2, P, PACK], BF16, name="wa_low", align_bytes=64)
+        wa_high = [keep.tile([P, 2, P // 2, PACK], BF16, name=f"wa_high{u}", tag=tag, align_bytes=64) for u, tag in enumerate(("cast_v", "cast_s"))]
+        nc.vector.tensor_copy(wa_low[:].rearrange("p t m j -> p m j t"), wa_src[:, :, :, 0:2])
+        nc.vector.tensor_copy(wa_high[0][:].rearrange("p t m j -> p m j t"), wa_src[:, 0 : P // 2, :, 2:4])
+        nc.scalar.copy(wa_high[1][:].rearrange("p t m j -> p m j t"), wa_src[:, P // 2 : P, :, 2:4])
 
         wa_codes = keep.tile([P, F], U32, name="wa_codes", align_bytes=64)
         wa_scales = keep.tile([P, F], U8, name="wa_scales", align_bytes=64)
+
+        def quantise_wa(lo, src):
+            cols = slice(lo, lo + src.shape[1] // PACK)
+            nc.vector.quantize_mx(out=wa_codes[:, cols].bitcast(FP8X4), scales=wa_scales[:, cols], in_=src)
+
+        quantise_wa(0, wa_low[:].rearrange("p t m j -> p (t m j)"))
         for u in range(2):
-            cols = slice(2 * P * u, 2 * P * (u + 1))
-            nc.vector.quantize_mx(
-                out=wa_codes[:, cols].bitcast(FP8X4),
-                scales=wa_scales[:, cols],
-                in_=wa_bf[u][:].rearrange("p t m j -> p (t m j)"),
-            )
+            for t in range(2):
+                quantise_wa((2 + t) * P + u * (P // 2), wa_high[u][:, t].rearrange("p m j -> p (m j)"))
 
         xf_last = keep.tile([P, T], F32, name="xf_last", tag="cast_s", align_bytes=64)
         nc.gpsimd.memset(xf_last[:], 0.0)
@@ -165,14 +169,16 @@ def tile_attend_depthffn_kernel(tc, tok_words, tok_scales, wa, wb, rw, res, offs
         nc.vector.tensor_tensor(x_half[0][:], o_first[:], rw_flat[:, 0:HALF], ALU.mult)
         quantise_h(3)
         for c, bank in ((2, "bank_z0"), (3, "banks_b")):
-            o_chunk = keep.tile([P, CHUNK], F32, name=f"o_chunk{c}")
+            o_chunk = keep.tile([P, CHUNK], F32, name=f"o_chunk{c}", tag=f"o_chunk{c}")
             nc.scalar.copy(o_chunk[:], second_layer(0, c * CHUNK, CHUNK, bank)[:])
             dst = x_half[1][:, c * CHUNK - HALF : (c + 1) * CHUNK - HALF]
             nc.gpsimd.tensor_tensor(dst, o_chunk[:], rw_flat[:, c * CHUNK : (c + 1) * CHUNK], ALU.mult)
-        o_last = keep.tile([P, I], F32, name="o_last", tag="pool_io")
-        nc.scalar.copy(o_last[:], second_layer(1, 0, I, "bank_c")[:])
-        x_last = keep.tile([P, I], F32, name="x_last")
-        nc.gpsimd.tensor_tensor(x_last[:], o_last[:], rw_flat, ALU.mult)
+        x_last = keep.tile([P, I], F32, name="x_last", tag="o_chunk3")
+        for h, (bank, tag) in enumerate((("bank_z1", "o_last0"), ("bank_c", "pool_io"))):
+            cols = slice(h * HALF, (h + 1) * HALF)
+            o_last = keep.tile([P, HALF], F32, name=f"o_last{h}", tag=tag)
+            nc.scalar.copy(o_last[:], second_layer(1, h * HALF, HALF, bank)[:])
+            nc.gpsimd.tensor_tensor(x_last[:, cols], o_last[:], rw_flat[:, cols], ALU.mult)
 
         def turn_onto(acc, src, lo, hi, opens):
             blocks = (hi - lo) // P

@@ -65,6 +65,8 @@ def tile_attend_depthffn_kernel(tc, tok_words, tok_scales, wa, wb, rw, res, offs
         nc.vector.memset(ident[:], 0.0)
         nc.vector.memset(xf_first[:], 0.0)
         make_identity(nc, ident[:], nomemset=True)
+        xf_last = keep.tile([P, T], F32, name="xf_last")
+        nc.vector.memset(xf_last[:], 0.0)
 
         rw_ps = psum.tile([P, PACK, P], F32, name="rw_ps", tag="bank_a")
         for j in range(PACK):
@@ -92,8 +94,6 @@ def tile_attend_depthffn_kernel(tc, tok_words, tok_scales, wa, wb, rw, res, offs
             for t in range(2):
                 quantise_wa((2 + t) * P + u * (P // 2), wa_high[u][:, t].rearrange("p m j -> p (m j)"))
 
-        xf_last = keep.tile([P, T], F32, name="xf_last", tag="cast_s", align_bytes=64)
-        nc.gpsimd.memset(xf_last[:], 0.0)
         res_first = keep.tile([P, T], F32, name="res_first", tag="gathered", align_bytes=64)
         nc.sync.dma_start(res_first[:], res[0:P, :])
 

@@ -18,13 +18,11 @@ ALU = mybir.AluOpType
 
 P = 128
 PACK = 4
-HALF = I // 2
+GROUP = 16
 CHUNK = 128
-LIST_COLS = HALF // 16
+HALF = I // 2
 
-POOL_COLS = [(0, 256), (256, 576), (576, 896), (896, 1152)]
-TURN_COLS = [(1152, 1408), (1408, 1792), (1792, 2048)]
-LAST_COLS = [(0, 384), (384, 896), (896, 1472), (1472, 2048)]
+PIECES = ((0, 320, 832, 1408, 2048), (0, 640, 1344, 2048))
 
 
 def tile_attend_depthffn_kernel(tc, tok_words, tok_scales, wa, wb, rw, res, offs, out):
@@ -33,8 +31,11 @@ def tile_attend_depthffn_kernel(tc, tok_words, tok_scales, wa, wb, rw, res, offs
         keep = ctx.enter_context(tc.tile_pool(name="keep", bufs=1))
         psum = ctx.enter_context(tc.psum_pool(name="psum", bufs=1))
 
-        offsets = keep.tile([P, I // 16], U16, name="offsets")
+        offsets = keep.tile([P, I // GROUP], U16, name="offsets")
         rw_cols = keep.tile([P, PACK], F32, name="rw_cols", tag="cast_s", align_bytes=64)
+
+        def listed(lo, n):
+            return offsets[:, lo // GROUP : (lo + n) // GROUP]
 
         scale_pool = keep.tile([P, T], U8, name="scale_pool", tag="scales", align_bytes=64)
         nc.gpsimd.memset(scale_pool[:].bitcast(I32), 0)
@@ -60,15 +61,15 @@ def tile_attend_depthffn_kernel(tc, tok_words, tok_scales, wa, wb, rw, res, offs
         wb_raw = keep.tile([P, PACK, E], F32, name="wb_raw", tag="scales", align_bytes=64)
         nc.sync.dma_start(wb_raw[:], wb.rearrange("(p j) e -> p j e", j=PACK))
 
-        xf_first = keep.tile([P, T], F32, name="xf_first")
         ident = keep.tile([P, P], F32, name="ident")
+        window = [keep.tile([P, T], F32, name=f"window{g}") for g in range(2)]
         nc.vector.memset(ident[:], 0.0)
-        nc.vector.memset(xf_first[:], 0.0)
+        nc.vector.memset(window[0][:], 0.0)
         make_identity(nc, ident[:], nomemset=True)
-        xf_last = keep.tile([P, T], F32, name="xf_last")
-        nc.vector.memset(xf_last[:], 0.0)
+        nc.vector.memset(window[1][:, 0 : T // 2], 0.0)
+        nc.gpsimd.memset(window[1][:, T // 2 : T], 0.0)
 
-        rw_ps = psum.tile([P, PACK, P], F32, name="rw_ps", tag="bank_a")
+        rw_ps = psum.tile([P, PACK, P], F32, name="rw_ps", tag="bank_o00")
         for j in range(PACK):
             nc.tensor.transpose(rw_ps[:, j, :], rw_cols[:, j : j + 1].to_broadcast([P, P]), ident[:])
         rw_rows = keep.tile([P, P, PACK], F32, name="rw_rows")
@@ -77,7 +78,10 @@ def tile_attend_depthffn_kernel(tc, tok_words, tok_scales, wa, wb, rw, res, offs
 
         wa_src = wa_raw[:].rearrange("p j (m t) -> p m j t", t=PACK)
         wa_low = keep.tile([P, 2, P, PACK], BF16, name="wa_low", align_bytes=64)
-        wa_high = [keep.tile([P, 2, P // 2, PACK], BF16, name=f"wa_high{u}", tag=tag, align_bytes=64) for u, tag in enumerate(("cast_v", "cast_s"))]
+        wa_high = [
+            keep.tile([P, 2, P // 2, PACK], BF16, name=f"wa_high{u}", tag=tag, align_bytes=64)
+            for u, tag in enumerate(("cast_v", "cast_s"))
+        ]
         nc.vector.tensor_copy(wa_low[:].rearrange("p t m j -> p m j t"), wa_src[:, :, :, 0:2])
         nc.vector.tensor_copy(wa_high[0][:].rearrange("p t m j -> p m j t"), wa_src[:, 0 : P // 2, :, 2:4])
         nc.scalar.copy(wa_high[1][:].rearrange("p t m j -> p m j t"), wa_src[:, P // 2 : P, :, 2:4])
@@ -85,24 +89,25 @@ def tile_attend_depthffn_kernel(tc, tok_words, tok_scales, wa, wb, rw, res, offs
         wa_codes = keep.tile([P, F], U32, name="wa_codes", align_bytes=64)
         wa_scales = keep.tile([P, F], U8, name="wa_scales", align_bytes=64)
 
-        def quantise_wa(lo, src):
+        def quantise(codes, scales, lo, src):
             cols = slice(lo, lo + src.shape[1] // PACK)
-            nc.vector.quantize_mx(out=wa_codes[:, cols].bitcast(FP8X4), scales=wa_scales[:, cols], in_=src)
+            nc.vector.quantize_mx(out=codes[:, cols].bitcast(FP8X4), scales=scales[:, cols], in_=src)
 
-        quantise_wa(0, wa_low[:].rearrange("p t m j -> p (t m j)"))
+        quantise(wa_codes, wa_scales, 0, wa_low[:].rearrange("p t m j -> p (t m j)"))
         for u in range(2):
             for t in range(2):
-                quantise_wa((2 + t) * P + u * (P // 2), wa_high[u][:, t].rearrange("p m j -> p (m j)"))
+                lo = (2 + t) * P + u * (P // 2)
+                quantise(wa_codes, wa_scales, lo, wa_high[u][:, t].rearrange("p m j -> p (m j)"))
 
-        res_first = keep.tile([P, T], F32, name="res_first", tag="gathered", align_bytes=64)
-        nc.sync.dma_start(res_first[:], res[0:P, :])
+        res_tile = [
+            keep.tile([P, T], F32, name=f"res{g}", tag=tag, align_bytes=64)
+            for g, tag in enumerate(("gathered", "scales"))
+        ]
+        nc.sync.dma_start(res_tile[0][:], res[0:P, :])
 
         tok_g = keep.tile([P, I], U32, name="tok_g", tag="wa", align_bytes=64)
-        for h in range(2):
-            nc.vector.tensor_copy(
-                tok_g[:, h * HALF : (h + 1) * HALF],
-                word_pool[:].indirect(offsets[:, h * LIST_COLS : (h + 1) * LIST_COLS]),
-            )
+        for lo in range(0, I, CHUNK):
+            nc.vector.tensor_copy(tok_g[:, lo : lo + CHUNK], word_pool[:].indirect(listed(lo, CHUNK)))
 
         h_bf = []
         for c in range(I // CHUNK):
@@ -119,7 +124,7 @@ def tile_attend_depthffn_kernel(tc, tok_words, tok_scales, wa, wb, rw, res, offs
                 )
             hb = keep.tile([P, CHUNK, PACK], BF16, name=f"h_bf{c}", align_bytes=64)
             h_bf.append(hb)
-            nc.scalar.activation(hb[:], z[:].rearrange("p t i -> p i t"), ACT.Relu, bias=xf_first[:, 0:1])
+            nc.scalar.activation(hb[:], z[:].rearrange("p t i -> p i t"), ACT.Relu)
 
         wb_codes = keep.tile([P, E], U32, name="wb_codes", align_bytes=64)
         wb_scales = keep.tile([P, E], U8, name="wb_scales", align_bytes=64)
@@ -131,103 +136,45 @@ def tile_attend_depthffn_kernel(tc, tok_words, tok_scales, wa, wb, rw, res, offs
         for g in range(2):
             dst = wb_bf[:, g * P : (g + 1) * P, :].rearrange("p (c i) j -> p c j i", i=PACK)
             nc.vector.tensor_copy(dst, wb_src[:, quads * g : quads * (g + 1)])
-        res_last = keep.tile([P, T], F32, name="res_last", tag="scales", align_bytes=64)
-        nc.sync.dma_start(res_last[:], res[P:E, :])
+        nc.sync.dma_start(res_tile[1][:], res[P:E, :])
         for g in range(2):
-            cols = slice(g * P, (g + 1) * P)
-            nc.vector.quantize_mx(
-                out=wb_codes[:, cols].bitcast(FP8X4),
-                scales=wb_scales[:, cols],
-                in_=wb_bf[:, cols, :].rearrange("p e j -> p (e j)"),
-            )
+            quantise(wb_codes, wb_scales, g * P, wb_bf[:, g * P : (g + 1) * P, :].rearrange("p e j -> p (e j)"))
 
         def quantise_h(c):
-            cols = slice(c * CHUNK, (c + 1) * CHUNK)
-            nc.vector.quantize_mx(
-                out=h_codes[:, cols].bitcast(FP8X4),
-                scales=h_scales[:, cols],
-                in_=h_bf[c][:].rearrange("p i t -> p (i t)"),
-            )
+            quantise(h_codes, h_scales, c * CHUNK, h_bf[c][:].rearrange("p i t -> p (i t)"))
 
-        def second_layer(g, lo, width, bank):
-            o = psum.tile([P, width], F32, name=f"o{g}_{lo}", tag=bank)
+        def weighted(g, h):
+            cols = slice(h * HALF, (h + 1) * HALF)
+            o = psum.tile([P, HALF], F32, name=f"o{g}{h}", tag=f"bank_o{g}{h}")
             nc.tensor.matmul_mx(
                 out=o[:],
                 lhsT=wb_codes[:, g * P : (g + 1) * P].bitcast(FP8X4),
                 lhsT_scale=wb_scales[:, g * P : (g + 1) * P],
-                rhs=h_codes[:, lo : lo + width].bitcast(FP8X4),
-                rhs_scale=h_scales[:, lo : lo + width],
+                rhs=h_codes[:, cols].bitcast(FP8X4),
+                rhs_scale=h_scales[:, cols],
                 start=True,
                 stop=True,
             )
-            return o
+            x = keep.tile([P, HALF], F32, name=f"x{g}{h}")
+            nc.vector.tensor_tensor(x[:], o[:], rw_flat[:, cols], ALU.mult)
+            return x
 
-        for c in range(3):
-            quantise_h(c)
-        x_half = [keep.tile([P, HALF], F32, name=f"x_half{h}") for h in range(2)]
-        o_first = second_layer(0, 0, HALF, "bank_a")
-        nc.vector.tensor_tensor(x_half[0][:], o_first[:], rw_flat[:, 0:HALF], ALU.mult)
+        quantise_h(0)
+        quantise_h(1)
+        quantise_h(2)
+        x00 = weighted(0, 0)
         quantise_h(3)
-        for c, bank in ((2, "bank_z0"), (3, "banks_b")):
-            o_chunk = keep.tile([P, CHUNK], F32, name=f"o_chunk{c}", tag=f"o_chunk{c}")
-            nc.scalar.copy(o_chunk[:], second_layer(0, c * CHUNK, CHUNK, bank)[:])
-            dst = x_half[1][:, c * CHUNK - HALF : (c + 1) * CHUNK - HALF]
-            nc.gpsimd.tensor_tensor(dst, o_chunk[:], rw_flat[:, c * CHUNK : (c + 1) * CHUNK], ALU.mult)
-        x_last = keep.tile([P, I], F32, name="x_last", tag="o_chunk3")
-        for h, (bank, tag) in enumerate((("bank_z1", "o_last0"), ("bank_c", "pool_io"))):
-            cols = slice(h * HALF, (h + 1) * HALF)
-            o_last = keep.tile([P, HALF], F32, name=f"o_last{h}", tag=tag)
-            nc.scalar.copy(o_last[:], second_layer(1, h * HALF, HALF, bank)[:])
-            nc.gpsimd.tensor_tensor(x_last[:, cols], o_last[:], rw_flat[:, cols], ALU.mult)
+        x10 = weighted(1, 0)
+        x01 = weighted(0, 1)
+        x11 = weighted(1, 1)
 
-        def turn_onto(acc, src, lo, hi, opens):
-            blocks = (hi - lo) // P
-            for k in range(blocks):
-                nc.tensor.matmul(
-                    acc[:, k * P : (k + 1) * P],
-                    src[:, lo + k * P : lo + (k + 1) * P],
-                    ident[:],
-                    start=(opens and k == 0),
-                    stop=(not opens and k == blocks - 1),
-                    is_transpose=True,
-                )
+        nc.scalar.activation(window[0][:].indirect(listed(0, HALF)), x00[:], ACT.Copy)
+        nc.vector.tensor_copy(window[0][:].indirect(listed(HALF, HALF)), x01[:])
+        nc.scalar.activation(window[1][:].indirect(listed(0, HALF)), x10[:], ACT.Copy)
+        nc.scalar.activation(window[1][:].indirect(listed(HALF, HALF)), x11[:], ACT.Copy)
 
-        def turn_back(b, turned_sum):
-            lo, hi = TURN_COLS[b]
-            back = psum.tile([P, hi - lo], F32, name=f"back{b}", tag=f"bank_z{b + 1}")
-            for k in range((hi - lo) // P):
-                nc.tensor.transpose(back[:, k * P : (k + 1) * P], turned_sum[:, k * P : (k + 1) * P], ident[:])
-            y_turn = keep.tile([P, hi - lo], F32, name=f"y_turn{b}")
-            nc.scalar.copy(y_turn[:], back[:])
-            nc.scalar.dma_start(out[0:P, lo:hi], y_turn[:])
-
-        two_banks = psum.tile([P, 2, I], F32, name="two_banks", tag="banks_b")
-        third_bank = psum.tile([P, I], F32, name="third_bank", tag="bank_c")
-        banks = [two_banks[:, 0, :], two_banks[:, 1, :], third_bank[:]]
-        turned = [banks[b][:, 0 : hi - lo] for b, (lo, hi) in enumerate(TURN_COLS)]
-        for b, (lo, hi) in enumerate(TURN_COLS):
-            turn_onto(turned[b], res_first, lo, hi, True)
-
-        for h in range(2):
-            nc.vector.tensor_copy(xf_first[:].indirect(offsets[:, h * LIST_COLS : (h + 1) * LIST_COLS]), x_half[h][:])
-        nc.vector.tensor_copy(xf_last[:].indirect(offsets[:]), x_last[:])
-
-        y_pool = keep.tile([P, POOL_COLS[-1][1]], F32, name="y_pool", tag="pool_io")
-        for lo, hi in POOL_COLS:
-            nc.gpsimd.tensor_tensor(y_pool[:, lo:hi], xf_first[:, lo:hi], res_first[:, lo:hi], ALU.add)
-            nc.sync.dma_start(out[0:P, lo:hi], y_pool[:, lo:hi])
-
-        sums = []
-        for b, (lo, hi) in enumerate(TURN_COLS):
-            turn_onto(turned[b], xf_first, lo, hi, False)
-            turned_sum = keep.tile([P, hi - lo], F32, name=f"turned_sum{b}")
-            nc.scalar.copy(turned_sum[:], turned[b])
-            sums.append(turned_sum)
-            if b > 0:
-                turn_back(b - 1, sums[b - 1])
-        turn_back(len(TURN_COLS) - 1, sums[-1])
-
-        for n, (lo, hi) in enumerate(LAST_COLS):
-            y_last = keep.tile([P, hi - lo], F32, name=f"y_last{n}")
-            nc.vector.tensor_tensor(y_last[:], xf_last[:, lo:hi], res_last[:, lo:hi], ALU.add)
-            nc.sync.dma_start(out[P:E, lo:hi], y_last[:])
+        for g in range(2):
+            for lo, hi in zip(PIECES[g], PIECES[g][1:]):
+                y = keep.tile([P, hi - lo], F32, name=f"y{g}_{lo}")
+                nc.vector.tensor_tensor(y[:], window[g][:, lo:hi], res_tile[g][:, lo:hi], ALU.add)
+                nc.sync.dma_start(out[g * P : (g + 1) * P, lo:hi], y[:])

@@ -122,7 +122,7 @@ def tile_attend_depthffn_kernel(tc, tok_words, tok_scales, wa, wb, rw, res, offs
                     start=True,
                     stop=True,
                 )
-            hb = keep.tile([P, CHUNK, PACK], BF16, name=f"h_bf{c}", align_bytes=64)
+            hb = keep.tile([P, CHUNK, PACK], BF16, name=f"h_bf{c}", tag=f"h_bf{c}", align_bytes=64)
             h_bf.append(hb)
             nc.scalar.activation(hb[:], z[:].rearrange("p t i -> p i t"), ACT.Relu)
 
@@ -143,9 +143,10 @@ def tile_attend_depthffn_kernel(tc, tok_words, tok_scales, wa, wb, rw, res, offs
         def quantise_h(c):
             quantise(h_codes, h_scales, c * CHUNK, h_bf[c][:].rearrange("p i t -> p (i t)"))
 
-        def weighted(g, h):
-            cols = slice(h * HALF, (h + 1) * HALF)
-            o = psum.tile([P, HALF], F32, name=f"o{g}{h}", tag=f"bank_o{g}{h}")
+        def weighted(dst, g, lo, bank):
+            width = dst.shape[1]
+            cols = slice(lo, lo + width)
+            o = psum.tile([P, width], F32, name=f"o{g}_{lo}", tag=bank)
             nc.tensor.matmul_mx(
                 out=o[:],
                 lhsT=wb_codes[:, g * P : (g + 1) * P].bitcast(FP8X4),
@@ -155,18 +156,18 @@ def tile_attend_depthffn_kernel(tc, tok_words, tok_scales, wa, wb, rw, res, offs
                 start=True,
                 stop=True,
             )
-            x = keep.tile([P, HALF], F32, name=f"x{g}{h}")
-            nc.vector.tensor_tensor(x[:], o[:], rw_flat[:, cols], ALU.mult)
-            return x
+            nc.vector.tensor_tensor(dst, o[:], rw_flat[:, cols], ALU.mult)
 
-        quantise_h(0)
-        quantise_h(1)
-        quantise_h(2)
-        x00 = weighted(0, 0)
+        x00 = keep.tile([P, HALF], F32, name="x00", tag="h_bf1", align_bytes=64)
+        x01, x10, x11 = (keep.tile([P, HALF], F32, name=name) for name in ("x01", "x10", "x11"))
+        for c in range(3):
+            quantise_h(c)
+        weighted(x00[:, 0:CHUNK], 0, 0, "bank_o00")
+        weighted(x00[:, CHUNK:HALF], 0, CHUNK, "bank_z0")
         quantise_h(3)
-        x10 = weighted(1, 0)
-        x01 = weighted(0, 1)
-        x11 = weighted(1, 1)
+        weighted(x10[:], 1, 0, "bank_o10")
+        weighted(x01[:], 0, HALF, "bank_o01")
+        weighted(x11[:], 1, HALF, "bank_o11")
 
         nc.scalar.activation(window[0][:].indirect(listed(0, HALF)), x00[:], ACT.Copy)
         nc.vector.tensor_copy(window[0][:].indirect(listed(HALF, HALF)), x01[:])

@@ -21,6 +21,7 @@ PACK = 4
 GROUP = 16
 CHUNK = 128
 HALF = I // 2
+BURST = 256
 
 PIECES = ((0, 320, 832, 1408, 2048), (0, 640, 1344, 2048))
 
@@ -37,29 +38,30 @@ def tile_attend_depthffn_kernel(tc, tok_words, tok_scales, wa, wb, rw, res, offs
         def listed(lo, n):
             return offsets[:, lo // GROUP : (lo + n) // GROUP]
 
-        scale_pool = keep.tile([P, T], U8, name="scale_pool", tag="scales", align_bytes=64)
+        scale_pool = keep.tile([P, T], U8, name="scale_pool", tag="scales", align_bytes=BURST)
         nc.gpsimd.memset(scale_pool[:].bitcast(I32), 0)
-        wa_raw = keep.tile([P, PACK, F], F32, name="wa_raw", tag="wa", align_bytes=64)
+        wa_raw = keep.tile([P, PACK, F], F32, name="wa_raw", tag="wa", align_bytes=BURST)
         wa_rows = wa.rearrange("(p j) f -> p j f", j=PACK)
         nc.sync.dma_start(wa_raw[:, 0:1, :], wa_rows[:, 0:1, :])
         nc.sync.dma_start(offsets[:], offs)
         nc.sync.dma_start(rw_cols[:], rw.rearrange("o (p j) -> (o p) j", j=PACK))
         nc.sync.dma_start(scale_pool[0:P:8, :].bitcast(I32), tok_scales[0].bitcast(I32))
         nc.sync.dma_start(wa_raw[:, 1:PACK, :], wa_rows[:, 1:PACK, :])
-        word_pool = keep.tile([P, T], U32, name="word_pool", tag="words", align_bytes=64)
+        word_pool = keep.tile([P, T], U32, name="word_pool", tag="words", align_bytes=BURST)
         nc.sync.dma_start(
             word_pool[:].bitcast(I32),
             tok_words[0].rearrange("p t r -> p (t r)").bitcast(I32),
         )
 
-        scale_g = keep.tile([P, I], U8, name="scale_g", tag="gathered", align_bytes=64)
+        scale_g = keep.tile([P, I], U8, name="scale_g", tag="gathered", align_bytes=BURST)
         nc.vector.tensor_copy(scale_g[:], scale_pool[:].indirect(offsets[:]))
-        tok_plane = keep.tile([P, I], U8, name="tok_plane", align_bytes=64)
+        tok_plane = keep.tile([P, I], U8, name="tok_plane", align_bytes=BURST)
         nc.gpsimd.memset(tok_plane[:].bitcast(I32), 0)
         for r in range(4):
             nc.sync.dma_start(tok_plane[r:P:32, :].bitcast(I32), scale_g[8 * r : P : 32, :].bitcast(I32))
-        wb_raw = keep.tile([P, PACK, E], F32, name="wb_raw", tag="scales", align_bytes=64)
-        nc.sync.dma_start(wb_raw[:], wb.rearrange("(p j) e -> p j e", j=PACK))
+        wb_raw = keep.tile([P, 2, PACK, P], F32, name="wb_raw", tag="scales", align_bytes=BURST)
+        for g in range(2):
+            nc.sync.dma_start(wb_raw[:, g], wb[:, g * P : (g + 1) * P].rearrange("(p j) e -> p j e", j=PACK))
 
         ident = keep.tile([P, P], F32, name="ident")
         window = [keep.tile([P, T], F32, name=f"window{g}") for g in range(2)]
@@ -100,12 +102,12 @@ def tile_attend_depthffn_kernel(tc, tok_words, tok_scales, wa, wb, rw, res, offs
                 quantise(wa_codes, wa_scales, lo, wa_high[u][:, t].rearrange("p m j -> p (m j)"))
 
         res_tile = [
-            keep.tile([P, T], F32, name=f"res{g}", tag=tag, align_bytes=64)
+            keep.tile([P, T], F32, name=f"res{g}", tag=tag, align_bytes=BURST)
             for g, tag in enumerate(("gathered", "scales"))
         ]
         nc.sync.dma_start(res_tile[0][:], res[0:P, :])
 
-        tok_g = keep.tile([P, I], U32, name="tok_g", tag="wa", align_bytes=64)
+        tok_g = keep.tile([P, I], U32, name="tok_g", tag="wa", align_bytes=BURST)
         for lo in range(0, I, CHUNK):
             nc.vector.tensor_copy(tok_g[:, lo : lo + CHUNK], word_pool[:].indirect(listed(lo, CHUNK)))
 
@@ -128,17 +130,14 @@ def tile_attend_depthffn_kernel(tc, tok_words, tok_scales, wa, wb, rw, res, offs
 
         wb_codes = keep.tile([P, E], U32, name="wb_codes", align_bytes=64)
         wb_scales = keep.tile([P, E], U8, name="wb_scales", align_bytes=64)
-        wb_src = wb_raw[:].rearrange("p j (c i) -> p c j i", i=PACK)
-        wb_bf = keep.tile([P, E, PACK], BF16, name="wb_bf", tag="words", align_bytes=64)
         h_codes = keep.tile([P, I], U32, name="h_codes", align_bytes=64)
         h_scales = keep.tile([P, I], U8, name="h_scales", align_bytes=64)
-        quads = P // PACK
-        for g in range(2):
-            dst = wb_bf[:, g * P : (g + 1) * P, :].rearrange("p (c i) j -> p c j i", i=PACK)
-            nc.vector.tensor_copy(dst, wb_src[:, quads * g : quads * (g + 1)])
-        nc.sync.dma_start(res_tile[1][:], res[P:E, :])
-        for g in range(2):
-            quantise(wb_codes, wb_scales, g * P, wb_bf[:, g * P : (g + 1) * P, :].rearrange("p e j -> p (e j)"))
+
+        def cast_wb(g, tag, align):
+            wb_bf = keep.tile([P, P, PACK], BF16, name=f"wb_bf{g}", tag=tag, align_bytes=align)
+            dst = wb_bf[:].rearrange("p (c i) j -> p c j i", i=PACK)
+            nc.vector.tensor_copy(dst, wb_raw[:, g].rearrange("p j (c i) -> p c j i", i=PACK))
+            return wb_bf[:].rearrange("p e j -> p (e j)")
 
         def quantise_h(c):
             quantise(h_codes, h_scales, c * CHUNK, h_bf[c][:].rearrange("p i t -> p (i t)"))
@@ -160,13 +159,19 @@ def tile_attend_depthffn_kernel(tc, tok_words, tok_scales, wa, wb, rw, res, offs
 
         x00 = keep.tile([P, HALF], F32, name="x00", tag="h_bf1", align_bytes=64)
         x01, x10, x11 = (keep.tile([P, HALF], F32, name=name) for name in ("x01", "x10", "x11"))
-        for c in range(3):
-            quantise_h(c)
+        quantise(wb_codes, wb_scales, 0, cast_wb(0, "words", BURST))
+        quantise_h(0)
+        wb_second = cast_wb(1, "h_bf0", 64)
+        nc.sync.dma_start(res_tile[1][:], res[P:E, :])
+        quantise_h(1)
+        quantise(wb_codes, wb_scales, P, wb_second)
+        quantise_h(2)
         weighted(x00[:, 0:CHUNK], 0, 0, "bank_o00")
-        weighted(x00[:, CHUNK:HALF], 0, CHUNK, "bank_z0")
+        weighted(x00[:, CHUNK:HALF], 0, CHUNK, "bank_o02")
         quantise_h(3)
         weighted(x10[:], 1, 0, "bank_o10")
-        weighted(x01[:], 0, HALF, "bank_o01")
+        weighted(x01[:, 0:CHUNK], 0, HALF, "bank_z0")
+        weighted(x01[:, CHUNK:HALF], 0, HALF + CHUNK, "bank_z1")
         weighted(x11[:], 1, HALF, "bank_o11")
 
         nc.scalar.activation(window[0][:].indirect(listed(0, HALF)), x00[:], ACT.Copy)
@@ -176,6 +181,6 @@ def tile_attend_depthffn_kernel(tc, tok_words, tok_scales, wa, wb, rw, res, offs
 
         for g in range(2):
             for lo, hi in zip(PIECES[g], PIECES[g][1:]):
-                y = keep.tile([P, hi - lo], F32, name=f"y{g}_{lo}")
+                y = keep.tile([P, hi - lo], F32, name=f"y{g}_{lo}", align_bytes=BURST)
                 nc.vector.tensor_tensor(y[:], window[g][:, lo:hi], res_tile[g][:, lo:hi], ALU.add)
                 nc.sync.dma_start(out[g * P : (g + 1) * P, lo:hi], y[:])

@@ -68,8 +68,7 @@ def tile_attend_depthffn_kernel(tc, tok_words, tok_scales, wa, wb, rw, res, offs
         nc.vector.memset(ident[:], 0.0)
         nc.vector.memset(window[0][:], 0.0)
         make_identity(nc, ident[:], nomemset=True)
-        nc.vector.memset(window[1][:, 0 : T // 2], 0.0)
-        nc.gpsimd.memset(window[1][:, T // 2 : T], 0.0)
+        nc.vector.memset(window[1][:], 0.0)
 
         rw_ps = psum.tile([P, PACK, P], F32, name="rw_ps", tag="bank_o00")
         for j in range(PACK):

@@ -39,7 +39,7 @@ def tile_attend_depthffn_kernel(tc, tok_words, tok_scales, wa, wb, rw, res, offs
             return offsets[:, lo // GROUP : (lo + n) // GROUP]
 
         scale_pool = keep.tile([P, T], U8, name="scale_pool", tag="scales", align_bytes=BURST)
-        nc.gpsimd.memset(scale_pool[:].bitcast(I32), 0)
+        nc.vector.memset(scale_pool[:].bitcast(I32), 0)
         wa_raw = keep.tile([P, PACK, F], F32, name="wa_raw", tag="wa", align_bytes=BURST)
         wa_rows = wa.rearrange("(p j) f -> p j f", j=PACK)
         nc.sync.dma_start(wa_raw[:, 0:1, :], wa_rows[:, 0:1, :])
@@ -65,10 +65,10 @@ def tile_attend_depthffn_kernel(tc, tok_words, tok_scales, wa, wb, rw, res, offs
 
         ident = keep.tile([P, P], F32, name="ident")
         window = [keep.tile([P, T], F32, name=f"window{g}") for g in range(2)]
-        nc.vector.memset(ident[:], 0.0)
         nc.vector.memset(window[0][:], 0.0)
-        make_identity(nc, ident[:], nomemset=True)
+        nc.vector.memset(ident[:], 0.0)
         nc.vector.memset(window[1][:], 0.0)
+        make_identity(nc, ident[:], nomemset=True)
 
         rw_ps = psum.tile([P, PACK, P], F32, name="rw_ps", tag="bank_o00")
         for j in range(PACK):
@@ -107,8 +107,8 @@ def tile_attend_depthffn_kernel(tc, tok_words, tok_scales, wa, wb, rw, res, offs
         nc.sync.dma_start(res_tile[0][:], res[0:P, :])
 
         tok_g = keep.tile([P, I], U32, name="tok_g", tag="wa", align_bytes=BURST)
-        for lo in range(0, I, CHUNK):
-            nc.vector.tensor_copy(tok_g[:, lo : lo + CHUNK], word_pool[:].indirect(listed(lo, CHUNK)))
+        for lo, count in ((0, CHUNK), (CHUNK, CHUNK), (HALF, HALF)):
+            nc.vector.tensor_copy(tok_g[:, lo : lo + count], word_pool[:].indirect(listed(lo, count)))
 
         h_bf = []
         for c in range(I // CHUNK):

@@ -42,11 +42,11 @@ def tile_attend_depthffn_kernel(tc, tok_words, tok_scales, wa, wb, rw, res, offs
         nc.vector.memset(scale_pool[:].bitcast(I32), 0)
         wa_raw = keep.tile([P, PACK, F], F32, name="wa_raw", tag="wa", align_bytes=BURST)
         wa_rows = wa.rearrange("(p j) f -> p j f", j=PACK)
-        nc.sync.dma_start(wa_raw[:, 0:1, :], wa_rows[:, 0:1, :])
+        nc.sync.dma_start(wa_raw[:, 0:2, :], wa_rows[:, 0:2, :])
         nc.sync.dma_start(offsets[:], offs)
         nc.sync.dma_start(rw_cols[:], rw.rearrange("o (p j) -> (o p) j", j=PACK))
         nc.sync.dma_start(scale_pool[0:P:8, :].bitcast(I32), tok_scales[0].bitcast(I32))
-        nc.sync.dma_start(wa_raw[:, 1:PACK, :], wa_rows[:, 1:PACK, :])
+        nc.sync.dma_start(wa_raw[:, 2:PACK, :], wa_rows[:, 2:PACK, :])
         word_pool = keep.tile([P, T], U32, name="word_pool", tag="words", align_bytes=BURST)
         nc.sync.dma_start(
             word_pool[:].bitcast(I32),
@@ -110,12 +110,11 @@ def tile_attend_depthffn_kernel(tc, tok_words, tok_scales, wa, wb, rw, res, offs
         for lo, count in ((0, CHUNK), (CHUNK, CHUNK), (HALF, HALF)):
             nc.vector.tensor_copy(tok_g[:, lo : lo + count], word_pool[:].indirect(listed(lo, count)))
 
-        h_bf = []
-        for c in range(I // CHUNK):
-            z = psum.tile([P, PACK, CHUNK], F32, name=f"z{c}", tag=f"bank_z{c}")
-            for t in range(PACK):
+        def first_layer(c, passes, bank):
+            z = psum.tile([P, len(passes), CHUNK], F32, name=f"z{c}_{passes[0]}", tag=bank)
+            for n, t in enumerate(passes):
                 nc.tensor.matmul_mx(
-                    out=z[:, t, :],
+                    out=z[:, n, :],
                     lhsT=wa_codes[:, t * P : (t + 1) * P].bitcast(FP8X4),
                     lhsT_scale=wa_scales[:, t * P : (t + 1) * P],
                     rhs=tok_g[:, c * CHUNK : (c + 1) * CHUNK].bitcast(FP8X4),
@@ -123,9 +122,14 @@ def tile_attend_depthffn_kernel(tc, tok_words, tok_scales, wa, wb, rw, res, offs
                     start=True,
                     stop=True,
                 )
-            hb = keep.tile([P, CHUNK, PACK], BF16, name=f"h_bf{c}", tag=f"h_bf{c}", align_bytes=64)
-            h_bf.append(hb)
-            nc.scalar.activation(hb[:], z[:].rearrange("p t i -> p i t"), ACT.Relu)
+            return z[:].rearrange("p t i -> p i t")
+
+        h_bf = [keep.tile([P, CHUNK, PACK], BF16, name=f"h_bf{c}", tag=f"h_bf{c}", align_bytes=64) for c in range(I // CHUNK)]
+        nc.scalar.activation(h_bf[0][:], first_layer(0, (0, 1, 2, 3), "bank_z0"), ACT.Relu)
+        z_pair = first_layer(1, (0, 1), "bank_z1")
+        nc.scalar.activation(h_bf[1][:, :, 2:4], first_layer(1, (2, 3), "bank_o11"), ACT.Relu)
+        nc.scalar.activation(h_bf[2][:], first_layer(2, (0, 1, 2, 3), "bank_z2"), ACT.Relu)
+        nc.scalar.activation(h_bf[3][:], first_layer(3, (0, 1, 2, 3), "bank_z3"), ACT.Relu)
 
         wb_codes = keep.tile([P, E], U32, name="wb_codes", align_bytes=64)
         wb_scales = keep.tile([P, E], U8, name="wb_scales", align_bytes=64)
@@ -158,18 +162,20 @@ def tile_attend_depthffn_kernel(tc, tok_words, tok_scales, wa, wb, rw, res, offs
 
         x00 = keep.tile([P, HALF], F32, name="x00", tag="h_bf1", align_bytes=64)
         x01, x10, x11 = (keep.tile([P, HALF], F32, name=name) for name in ("x01", "x10", "x11"))
-        quantise(wb_codes, wb_scales, 0, cast_wb(0, "words", BURST))
+        wb_first = cast_wb(0, "words", BURST)
+        nc.vector.tensor_scalar_max(h_bf[1][:, :, 0:2], z_pair, 0.0)
+        quantise(wb_codes, wb_scales, 0, wb_first)
         quantise_h(0)
+        quantise_h(1)
         wb_second = cast_wb(1, "h_bf0", 64)
         nc.sync.dma_start(res_tile[1][:], res[P:E, :])
-        quantise_h(1)
-        quantise(wb_codes, wb_scales, P, wb_second)
         quantise_h(2)
         weighted(x00[:, 0:CHUNK], 0, 0, "bank_o00")
         weighted(x00[:, CHUNK:HALF], 0, CHUNK, "bank_o02")
+        quantise(wb_codes, wb_scales, P, wb_second)
         quantise_h(3)
-        weighted(x10[:], 1, 0, "bank_o10")
         weighted(x01[:, 0:CHUNK], 0, HALF, "bank_z0")
+        weighted(x10[:], 1, 0, "bank_o10")
         weighted(x01[:, CHUNK:HALF], 0, HALF + CHUNK, "bank_z1")
         weighted(x11[:], 1, HALF, "bank_o11")
 

@@ -169,9 +169,9 @@ def tile_attend_depthffn_kernel(tc, tok_words, tok_scales, wa, wb, rw, res, offs
         quantise_h(1)
         wb_second = cast_wb(1, "h_bf0", 64)
         nc.sync.dma_start(res_tile[1][:], res[P:E, :])
-        quantise_h(2)
         weighted(x00[:, 0:CHUNK], 0, 0, "bank_o00")
         weighted(x00[:, CHUNK:HALF], 0, CHUNK, "bank_o02")
+        quantise_h(2)
         quantise(wb_codes, wb_scales, P, wb_second)
         quantise_h(3)
         weighted(x01[:, 0:CHUNK], 0, HALF, "bank_z0")

from contextlib import ExitStack

import concourse.mybir as mybir
from concourse.masks import make_identity

K, T, I, F, E = 512, 2048, 512, 512, 256
FLOPS = 2 * K * F * I + 2 * F * E * I

F32 = mybir.dt.float32
BF16 = mybir.dt.bfloat16
I32 = mybir.dt.int32
U32 = mybir.dt.uint32
U16 = mybir.dt.uint16
U8 = mybir.dt.uint8
FP8X4 = mybir.dt.float8_e4m3fn_x4
ACT = mybir.ActivationFunctionType
ALU = mybir.AluOpType

P = 128
PACK = 4
GROUP = 16
CHUNK = 128
HALF = I // 2
BURST = 256

PIECES = ((0, 320, 832, 1408, 2048), (0, 640, 1344, 2048))


def tile_attend_depthffn_kernel(tc, tok_words, tok_scales, wa, wb, rw, res, offs, out):
    nc = tc.nc
    with ExitStack() as ctx:
        keep = ctx.enter_context(tc.tile_pool(name="keep", bufs=1))
        psum = ctx.enter_context(tc.psum_pool(name="psum", bufs=1))

        offsets = keep.tile([P, I // GROUP], U16, name="offsets")
        rw_cols = keep.tile([P, PACK], F32, name="rw_cols", tag="cast_s", align_bytes=64)

        def listed(lo, n):
            return offsets[:, lo // GROUP : (lo + n) // GROUP]

        scale_pool = keep.tile([P, T], U8, name="scale_pool", tag="scales", align_bytes=BURST)
        nc.vector.memset(scale_pool[:].bitcast(I32), 0)
        wa_raw = keep.tile([P, PACK, F], F32, name="wa_raw", tag="wa", align_bytes=BURST)
        wa_rows = wa.rearrange("(p j) f -> p j f", j=PACK)
        nc.sync.dma_start(wa_raw[:, 0:2, :], wa_rows[:, 0:2, :])
        nc.sync.dma_start(offsets[:], offs)
        nc.sync.dma_start(rw_cols[:], rw.rearrange("o (p j) -> (o p) j", j=PACK))
        nc.sync.dma_start(scale_pool[0:P:8, :].bitcast(I32), tok_scales[0].bitcast(I32))
        nc.sync.dma_start(wa_raw[:, 2:PACK, :], wa_rows[:, 2:PACK, :])
        word_pool = keep.tile([P, T], U32, name="word_pool", tag="words", align_bytes=BURST)
        nc.sync.dma_start(
            word_pool[:].bitcast(I32),
            tok_words[0].rearrange("p t r -> p (t r)").bitcast(I32),
        )

        scale_g = keep.tile([P, I], U8, name="scale_g", tag="gathered", align_bytes=BURST)
        nc.vector.tensor_copy(scale_g[:], scale_pool[:].indirect(offsets[:]))
        tok_plane = keep.tile([P, I], U8, name="tok_plane", align_bytes=BURST)
        nc.gpsimd.memset(tok_plane[:].bitcast(I32), 0)
        for r in range(4):
            nc.sync.dma_start(tok_plane[r:P:32, :].bitcast(I32), scale_g[8 * r : P : 32, :].bitcast(I32))
        wb_raw = keep.tile([P, 2, PACK, P], F32, name="wb_raw", tag="scales", align_bytes=BURST)
        for g in range(2):
            nc.sync.dma_start(wb_raw[:, g], wb[:, g * P : (g + 1) * P].rearrange("(p j) e -> p j e", j=PACK))

        ident = keep.tile([P, P], F32, name="ident")
        window = [keep.tile([P, T], F32, name=f"window{g}") for g in range(2)]
        nc.vector.memset(window[0][:], 0.0)
        nc.vector.memset(ident[:], 0.0)
        nc.vector.memset(window[1][:], 0.0)
        make_identity(nc, ident[:], nomemset=True)

        rw_ps = psum.tile([P, PACK, P], F32, name="rw_ps", tag="bank_o00")
        for j in range(PACK):
            nc.tensor.transpose(rw_ps[:, j, :], rw_cols[:, j : j + 1].to_broadcast([P, P]), ident[:])
        rw_rows = keep.tile([P, P, PACK], F32, name="rw_rows")
        nc.scalar.copy(rw_rows[:], rw_ps[:].rearrange("p j n -> p n j"))
        rw_flat = rw_rows[:].rearrange("p n j -> p (n j)")

        wa_src = wa_raw[:].rearrange("p j (m t) -> p m j t", t=PACK)
        wa_low = keep.tile([P, 2, P, PACK], BF16, name="wa_low", align_bytes=64)
        wa_high = [
            keep.tile([P, 2, P // 2, PACK], BF16, name=f"wa_high{u}", tag=tag, align_bytes=64)
            for u, tag in enumerate(("cast_v", "cast_s"))
        ]
        nc.vector.tensor_copy(wa_low[:].rearrange("p t m j -> p m j t"), wa_src[:, :, :, 0:2])
        nc.vector.tensor_copy(wa_high[0][:].rearrange("p t m j -> p m j t"), wa_src[:, 0 : P // 2, :, 2:4])
        nc.scalar.copy(wa_high[1][:].rearrange("p t m j -> p m j t"), wa_src[:, P // 2 : P, :, 2:4])

        wa_codes = keep.tile([P, F], U32, name="wa_codes", align_bytes=64)
        wa_scales = keep.tile([P, F], U8, name="wa_scales", align_bytes=64)

        def quantise(codes, scales, lo, src):
            cols = slice(lo, lo + src.shape[1] // PACK)
            nc.vector.quantize_mx(out=codes[:, cols].bitcast(FP8X4), scales=scales[:, cols], in_=src)

        quantise(wa_codes, wa_scales, 0, wa_low[:].rearrange("p t m j -> p (t m j)"))
        for u in range(2):
            for t in range(2):
                lo = (2 + t) * P + u * (P // 2)
                quantise(wa_codes, wa_scales, lo, wa_high[u][:, t].rearrange("p m j -> p (m j)"))

        res_tile = [
            keep.tile([P, T], F32, name=f"res{g}", tag=tag, align_bytes=BURST)
            for g, tag in enumerate(("gathered", "scales"))
        ]
        nc.sync.dma_start(res_tile[0][:], res[0:P, :])

        tok_g = keep.tile([P, I], U32, name="tok_g", tag="wa", align_bytes=BURST)
        for lo, count in ((0, CHUNK), (CHUNK, CHUNK), (HALF, HALF)):
            nc.vector.tensor_copy(tok_g[:, lo : lo + count], word_pool[:].indirect(listed(lo, count)))

        def first_layer(c, passes, bank):
            z = psum.tile([P, len(passes), CHUNK], F32, name=f"z{c}_{passes[0]}", tag=bank)
            for n, t in enumerate(passes):
                nc.tensor.matmul_mx(
                    out=z[:, n, :],
                    lhsT=wa_codes[:, t * P : (t + 1) * P].bitcast(FP8X4),
                    lhsT_scale=wa_scales[:, t * P : (t + 1) * P],
                    rhs=tok_g[:, c * CHUNK : (c + 1) * CHUNK].bitcast(FP8X4),
                    rhs_scale=tok_plane[:, c * CHUNK : (c + 1) * CHUNK],
                    start=True,
                    stop=True,
                )
            return z[:].rearrange("p t i -> p i t")

        h_bf = [keep.tile([P, CHUNK, PACK], BF16, name=f"h_bf{c}", tag=f"h_bf{c}", align_bytes=64) for c in range(I // CHUNK)]
        nc.scalar.activation(h_bf[0][:], first_layer(0, (0, 1, 2, 3), "bank_z0"), ACT.Relu)
        z_pair = first_layer(1, (0, 1), "bank_z1")
        nc.scalar.activation(h_bf[1][:, :, 2:4], first_layer(1, (2, 3), "bank_o11"), ACT.Relu)
        nc.scalar.activation(h_bf[2][:], first_layer(2, (0, 1, 2, 3), "bank_z2"), ACT.Relu)
        nc.scalar.activation(h_bf[3][:], first_layer(3, (0, 1, 2, 3), "bank_z3"), ACT.Relu)

        wb_codes = keep.tile([P, E], U32, name="wb_codes", align_bytes=64)
        wb_scales = keep.tile([P, E], U8, name="wb_scales", align_bytes=64)
        h_codes = keep.tile([P, I], U32, name="h_codes", align_bytes=64)
        h_scales = keep.tile([P, I], U8, name="h_scales", align_bytes=64)

        def cast_wb(g, tag, align):
            wb_bf = keep.tile([P, P, PACK], BF16, name=f"wb_bf{g}", tag=tag, align_bytes=align)
            dst = wb_bf[:].rearrange("p (c i) j -> p c j i", i=PACK)
            nc.vector.tensor_copy(dst, wb_raw[:, g].rearrange("p j (c i) -> p c j i", i=PACK))
            return wb_bf[:].rearrange("p e j -> p (e j)")

        def quantise_h(c):
            quantise(h_codes, h_scales, c * CHUNK, h_bf[c][:].rearrange("p i t -> p (i t)"))

        def weighted(dst, g, lo, bank):
            width = dst.shape[1]
            cols = slice(lo, lo + width)
            o = psum.tile([P, width], F32, name=f"o{g}_{lo}", tag=bank)
            nc.tensor.matmul_mx(
                out=o[:],
                lhsT=wb_codes[:, g * P : (g + 1) * P].bitcast(FP8X4),
                lhsT_scale=wb_scales[:, g * P : (g + 1) * P],
                rhs=h_codes[:, cols].bitcast(FP8X4),
                rhs_scale=h_scales[:, cols],
                start=True,
                stop=True,
            )
            nc.vector.tensor_tensor(dst, o[:], rw_flat[:, cols], ALU.mult)

        x00 = keep.tile([P, HALF], F32, name="x00", tag="h_bf1", align_bytes=64)
        x01, x10, x11 = (keep.tile([P, HALF], F32, name=name) for name in ("x01", "x10", "x11"))
        wb_first = cast_wb(0, "words", BURST)
        nc.vector.tensor_scalar_max(h_bf[1][:, :, 0:2], z_pair, 0.0)
        quantise(wb_codes, wb_scales, 0, wb_first)
        quantise_h(0)
        quantise_h(1)
        wb_second = cast_wb(1, "h_bf0", 64)
        nc.sync.dma_start(res_tile[1][:], res[P:E, :])
        weighted(x00[:, 0:CHUNK], 0, 0, "bank_o00")
        weighted(x00[:, CHUNK:HALF], 0, CHUNK, "bank_o02")
        quantise_h(2)
        quantise(wb_codes, wb_scales, P, wb_second)
        quantise_h(3)
        weighted(x01[:, 0:CHUNK], 0, HALF, "bank_z0")
        weighted(x10[:], 1, 0, "bank_o10")
        weighted(x01[:, CHUNK:HALF], 0, HALF + CHUNK, "bank_z1")
        weighted(x11[:], 1, HALF, "bank_o11")

        nc.scalar.activation(window[0][:].indirect(listed(0, HALF)), x00[:], ACT.Copy)
        nc.vector.tensor_copy(window[0][:].indirect(listed(HALF, HALF)), x01[:])
        nc.scalar.activation(window[1][:].indirect(listed(0, HALF)), x10[:], ACT.Copy)
        nc.scalar.activation(window[1][:].indirect(listed(HALF, HALF)), x11[:], ACT.Copy)

        for g in range(2):
            for lo, hi in zip(PIECES[g], PIECES[g][1:]):
                y = keep.tile([P, hi - lo], F32, name=f"y{g}_{lo}", align_bytes=BURST)
                nc.vector.tensor_tensor(y[:], window[g][:, lo:hi], res_tile[g][:, lo:hi], ALU.add)
                nc.sync.dma_start(out[g * P : (g + 1) * P, lo:hi], y[:])
